import numpy as np, ml_dtypes
CORES = [5,29,101,125,133,157,229,253]
N = 8
BF = ml_dtypes.bfloat16
S, J, RO = 384, 1, 2
SH, HALF, QLO, QHI = 11, 1024, 512, 1536
B0, B1, B2, W = 4, 4, 3, 2048
def pack(pos, pf, rf, th, lv):
    turn = lambda a: np.ascontiguousarray(a.transpose(0, 1, 3, 2)).astype(np.float32).astype(BF)
    return {"pos": turn(pos).reshape(N, 24, S), "pf": turn(pf).reshape(N, 128, S), "rf": turn(rf).reshape(N, 128, W),
            "th": np.ascontiguousarray(th.reshape(N, 128, 1)).astype(np.int32), "lv": np.ascontiguousarray(lv.reshape(N, 8, S)).astype(np.int32)}
def parts(rng):
    pos = rng.integers(-31, 32, (N, 8, S, 3)); pf = rng.integers(0, 16, (N, 8, S, 16)); rf = rng.integers(-15, 16, (N, 8, W, 16)); th = rng.integers(0, 301, (N, 8, 16))
    share = rng.choice(np.array([0.8, 0.9, 1.0]), (N, 8, 1))
    return pos, pf, rf, th, (rng.random((N, 8, S)) < share).astype(np.int64)
def setup_inputs(rng):
    pos, pf, rf, th, lv = parts(rng); g = int(rng.integers(0, 8))
    lv[:, g] = rng.random((N, S)) < 0.07
    return pack(pos, pf, rf, th, lv)
def setup_inputs_spread(rng):
    pos, pf, rf, th, lv = parts(rng)
    pos = np.rint(rng.choice(np.array([2, 6, 13, 22, 31, 31, 31, 31]), (N, 8, S, 1)) * (2 * rng.random(pos.shape) - 1)).astype(np.int64)
    pf = np.minimum(np.floor(16 * rng.random(pf.shape) ** rng.choice(np.array([0.25, 1.0, 4.0]), (N, 8, S, 1))), 15).astype(np.int64)
    c = rng.choice(np.array([0, 1, 4, 15]), (N, 8, W, 1)); rf = np.clip(rf, -c, c)
    th = np.clip(np.where(rng.random(th.shape) < 0.5, -1, 1) * np.exp2(12 * rng.random(th.shape)).astype(np.int64), -3600, 3600)
    return pack(pos, pf, rf, th, lv)
def setup_inputs_ends(rng):
    pos = 31 * (2 * rng.integers(0, 2, (N, 8, S, 3)) - 1)
    loose = rng.random((N, 8, S, 1)) < 0.25; loose[:, 7] = False
    pos = np.where(loose, rng.integers(-31, 32, pos.shape), pos)
    u = rng.random((N, 8, S, 1)); pf = np.where(u < 0.45, 15, np.where(u < 0.6, 0, 15 * rng.integers(0, 2, (N, 8, S, 16))))
    u = rng.random((N, 8, W, 1)); c = rng.choice(np.array([0.15, 0.25, 0.35]), (N, 8, 1, 1))
    rf = np.where(u < c, 15, np.where(u > 0.75, -15, 30 * rng.integers(0, 2, (N, 8, W, 16)) - 15))
    lv = (rng.random((N, 8, S)) < 0.85).astype(np.int64); lv[:, 7] = 1; lv[:, :, S - 1] = 1
    th = np.full((N, 8, 16), 3600, np.int64); e = int(rng.integers(0, 7))
    th[:, e] = np.where(rng.random((N, 16)) < 0.5, -3600, 3600); th[:, 7, 15] = -3600; th[:, 7, int(rng.integers(0, 7)) * 2] = -3600
    for a in range(N):
        for g in range(8):
            on = np.flatnonzero(lv[a, g])[45:48]; pos[a, g, on] = 31 * np.array([[1, 1, -1], [1, -1, 1], [-1, 1, 1]])
    pos[:, :, S - 1] = 9; pf[:, :, S - 1] = 15; rf[:, :, W - 1] = 15
    return pack(pos, pf, rf, th, lv)
def setup_inputs_corners(rng):
    pos, pf, rf, th, lv = parts(rng)
    n_ = np.array([0, 1, 2, 3, 4, 5, 46, 47, 48, 49, S - 1, S])[rng.permutation(12)]
    for a in range(N):
        for g in range(8):
            n = int(n_[(8 * a + g) % 12]); w = int(rng.integers(0, 3))
            on = np.arange(n) if w == 0 else (np.arange(S - n, S) if w == 1 else rng.permutation(S)[:n])
            lv[a, g] = 0; lv[a, g, on] = 1
    u = rng.random((N, 8, S, 1)); pf = np.where(u < 0.2, 0, np.where(u > 0.9, 15, pf))
    th = rng.choice(np.array([0, 0, 1, 1, 100, 200, 300, 3600]), (N, 8, 16)); e = rng.permutation(8)[:2]
    th[:, e] = rng.choice(np.array([-3600, -1, 0, 300, 3600]), (N, 2, 16))
    return pack(pos, pf, rf, th, lv)
def setup_inputs_crowd(rng):
    pos, pf, rf, th, lv = parts(rng); lv[:] = 1; gp = rng.permutation(8); m = np.arange(16)
    rf[:, :, 0, :8] = 15; rf[:, :, 0, 8:] = -15
    one = int(rng.integers(0, N)); ms = int(rng.integers(1, 16))
    for i in range(8):
        g = int(gp[i]); m0 = int(rng.integers(1, 16) if i == 0 else rng.integers(0, 16 if i < 4 else 17))
        if i == 4: m0 = (ms + 1 + int(rng.integers(0, 15))) % 16
        for a in range(N):
            if i == 0: n = 0
            elif i == 1: n = a % 4
            elif i < 4: n = 2 + (a >> 1) % 2 if a % 2 == i - 2 else S // 2
            elif i == 4: n = 1 if a == one else 0
            else: n = int(rng.choice(np.array([1, 3, 47, 48, 49, S // 2])))
            o = np.concatenate([np.arange(48), 48 + rng.permutation(S - 48)]); herd, left = o[:S - n], o[S - n:]
            pos[a, g, herd] = rng.integers(-5, 6, (1, 3)) * rng.integers(-6, 7, (S - n, 1))
            b = np.zeros((S - n, 16), np.int64); b[:, :8] = rng.integers(3, 16, (S - n, 8))
            w = int(rng.integers(2 if i == 4 else 1, 16)); b[-1] = 0; b[-1, 0] = w
            pf[a, g, herd] = b
            x = rng.integers(0, 11, (n, 8)); pf[a, g, left] = np.concatenate([x, x + rng.integers(0, 6, (n, 8))], axis=1)
            v = int(rng.integers(1, w)) if i == 4 else 0
            first = 0 if i == 0 and a != one else m0
            th[a, g] = np.where(m < first, 15 * w + 1, rng.integers(15 * v + 1, 15 * w + 1, 16))
            if m0 < 16: th[a, g, m0] = 15 * w
            if i == 4:
                th[a, g, ms] = 15 * v; pf[a, g, left] = 0; pf[a, g, left, 0] = v
                pos[a, g, 48:, 0] = 5 * (2 * rng.integers(0, 2, S - 48) - 1); pos[a, g, 3 * ms:3 * ms + 3] = 16 * np.eye(3, dtype=np.int64)
    return pack(pos, pf, rf, th, lv)
def setup_inputs_ties(rng):
    pos, pf, rf, th, lv = parts(rng); gp = rng.permutation(8)
    base = rng.integers(0, 16, (N, 8, 1, 15)); o = np.argsort(rng.random((N, 8, S, 15)), axis=-1)
    pf[..., :15] = np.take_along_axis(np.broadcast_to(base, (N, 8, S, 15)), o, 3); pf[..., 15] = 1
    b = rng.choice(np.array([15, 14, 13, -15]), (N, 8, 1, 1)); rf[..., :15] = b; rf[..., 15] = rng.integers(-1, 2, (N, 8, W))
    th = (b * np.sum(base, axis=-1, keepdims=True)).reshape(N, 8, 1) + rng.integers(0, 2, (N, 8, 16))
    four = gp[3:6]; pos[:, four] = 4 * rng.integers(-7, 8, (N, 3, S, 3))
    up = ((HALF + 4096 >> SH) & 15) << (B1 + B2); dn = ((HALF - 4096 >> SH) & 15) << (B1 + B2)
    for i in range(3):
        g = int(gp[i])
        for a in range(N):
            kind = rng.integers(0, 2, 16); kind[0] = i % 2; kind[15] = 1 - i % 2
            pos[a, g] = 0; pf[a, g] = 0; lv[a, g] = 1; th[a, g] = rng.integers(1, 361, 16)
            pos[a, g, :48] = (16 * np.eye(3, dtype=np.int64)[None] * kind[:, None, None]).reshape(48, 3)
            x = 48 + rng.permutation(S - 48); h = (S - 48) // 2; one, two = x[:h], x[h:]
            pos[a, g, one, 0] = 16; pos[a, g, two, 0] = -16
            pf[a, g, one, :8] = rng.integers(3, 16, (h, 8)); pf[a, g, two, 8:] = rng.integers(3, 16, (S - 48 - h, 8))
            if i == 2 and a % 2 == 1: pf[a, g, one[0]] = 0
            rf[a, g, 0, :8] = 15; rf[a, g, 0, 8:] = 0; rf[a, g, up] = 0; rf[a, g, dn, :8] = 0; rf[a, g, dn, 8:] = 15
    g = int(gp[6]); s1 = 1 - 2 * ((np.arange(N) + int(rng.integers(0, 2))) % 2); lv[:, g] = 1
    pf[:, g] = 15; pf[:, g, :, 15] = rng.choice(np.array([1, 14, 15]), (N, S)); pf[:, g, S - 1, 15] = 14
    rf[:, g] = 15 * s1[:, None, None]
    rf[:, g, 1:, 15] = np.where(rng.random((N, W - 1)) < 0.4, 15 * s1[:, None], rng.choice(np.array([-14, -1, 0, 1, 14]), (N, W - 1)))
    th[:, g] = np.where(s1[:, None] > 0, rng.choice(np.array([3375, 3376, 3390, 3391, 3585, 3586, 3600]), (N, 16)), rng.choice(np.array([-3599, -3586, -3585, -3584, -3390, -3389, -3375]), (N, 16)))
    th[:, g, 15] = np.where(s1 > 0, 3586, -3585); th[:, g, 14] = np.where(s1 > 0, 3585, -3584)
    flat = rng.random((N, 16)) < 0.4; flat[:, 14:] = True
    pos[:, g, :48] = np.where(np.repeat(flat, 3, axis=1)[..., None], 0, pos[:, g, :48])
    g = int(gp[7]); lv[:, g] = 1; k = int(rng.integers(16, 31)); mm = int(rng.integers(0, 15))
    tri = np.array([[0, 0, 0], [k + 1, 31, -31], [k, 31, 31]]); e = np.arange(-31, 32)
    grid = np.stack(np.meshgrid(e, e, e, indexing="ij"), axis=-1).reshape(-1, 3)
    y = np.matmul(grid, np.cross(tri[1], tri[2])) + HALF
    c1 = y & (2 * HALF - 1); c2 = (y - grid[:, 0]) & (2 * HALF - 1)
    edge = grid[(c1 >= QLO) & (c1 < QHI) & ((c2 < QLO) | (c2 >= QHI))]
    pos[:, g, 45:48] = tri; pos[:, g, 3 * mm:3 * mm + 3] = tri[[0, 2, 1]]
    for a in range(N):
        x = np.append(48 + rng.permutation(S - 49)[:S // 4], S - 1); pos[a, g, x] = edge[rng.integers(0, len(edge), len(x))]
    th[:, g, mm] = -3600; th[:, g, 15] = -3600
    return pack(pos, pf, rf, th, lv)
def check_inputs(d):
    bad = []
    for k, lo, hi in (("pos", -31, 31), ("pf", 0, 15), ("rf", -15, 15), ("th", -3600, 3600), ("lv", 0, 1)):
        v = np.asarray(d[k]).astype(np.float32)
        if not (np.min(v) >= lo and np.max(v) <= hi): bad.append("range of " + k)
        if not np.all(np.floor(v) == v): bad.append("whole numbers in " + k)
    return bad
def judge(ax, P, I, R, T):
    y = np.matmul(ax, P[:, None]) + HALF
    c = y & (2 * HALF - 1); inside = np.all((c >= QLO) & (c < QHI), axis=2); n = y >> SH
    place = ((n[:, :, 0] & (2 ** B0 - 1)) << (B1 + B2)) + ((n[:, :, 1] & (2 ** B1 - 1)) << B2) + (n[:, :, 2] & (2 ** B2 - 1))
    score = np.add.reduce(R[np.arange(8)[:, None, None], place] * I[:, None], axis=-1)
    return inside & (score >= T)
def reference(pos, pf, rf, th, lv):
    P = pos.astype(np.float32).astype(np.int64).reshape(N, 8, 3, S)
    I = np.ascontiguousarray(pf.astype(np.float32).astype(np.int32).reshape(N, 8, 16, S).transpose(0, 1, 3, 2))
    R = np.ascontiguousarray(rf.astype(np.float32).astype(np.int32).reshape(N, 8, 16, W).transpose(0, 1, 3, 2))
    T = th.astype(np.int64).reshape(N, 8, 16, 1); live = lv.reshape(N, 8, S) != 0
    age = live.astype(np.int64); counts = []
    for t in range(RO):
        order = np.argsort(np.where(live, 0, 1), axis=-1, kind="stable")[..., :48]
        there = np.arange(48) < np.add.reduce(live, axis=-1, dtype=np.int64)[..., None]
        seed = (np.take_along_axis(P, order[:, :, None, :], 3) * there[:, :, None, :]).transpose(0, 1, 3, 2)
        p, q, s = seed[:, :, 0::3], seed[:, :, 1::3], seed[:, :, 2::3]
        ax = np.stack([np.cross(q, s), np.cross(s, p), np.cross(p, q)], axis=3)
        cnt = np.zeros((N, 8, 16), np.int64); hits = []
        for a in range(N):
            for i in range(J + 1):
                b = a if i == 0 else (a + t * J + i) % N
                h = judge(ax[a], P[b], I[b], R[b], T[b]); hits.append((a, b, h))
                cnt[a] = cnt[a] + np.add.reduce(h & live[b][:, None, :], axis=-1, dtype=np.int64)
        win = np.argmax(cnt, axis=2)
        die = np.zeros((N, 8, S), bool)
        for a, b, h in hits: die[b] = die[b] | h[np.arange(8), win[a]]
        live = live & ~die; age = age + live; counts.append(cnt)
    return {"yc": np.stack(counts, axis=-1).reshape(N, 128, RO).astype(np.float32), "ya": age.astype(np.float32)}

@@ -1,0 +1,462 @@
+from concourse.mybir import AluOpType as ALU, AxisListType as AX, ActivationFunctionType as AF
+
+S = 384
+RO = 2
+XA = 240
+XD = S - XA
+CH = [(0, 128), (128, XA)]
+COEF = [128.0, 8.0, 1.0]
+MOD = [16.0, 16.0, 8.0]
+BIG = 8192.0
+TW = 56
+POOL_PRE, POOL_POST = 5, 6
+
+SCRATCH = {
+    "posb": ("sbuf", [128, S], "bfloat16"), "lvi": ("sbuf", [128, S], "int32"), "lvb": ("sbuf", [128, S], "bfloat16"),
+    "pfb": ("sbuf", [128, S], "bfloat16"), "rfb": ("sbuf", [128, 2048], "bfloat16"),
+    "thi": ("sbuf", [128, 8], "int32"), "thf": ("sbuf", [128, 8], "float32"), "thc": ("sbuf", [128, 8], "float32"),
+    "wa": ("sbuf", [128, 400], "bfloat16"), "wb": ("sbuf", [128, 400], "bfloat16"), "posr": ("sbuf", [128, S], "float16"),
+    "pfx": ("sbuf", [128, 16 * XD], "bfloat16"),
+    "qp": ("sbuf", [128, 48], "float32"), "qm": ("sbuf", [128, 48], "float32"), "sel": ("sbuf", [128, 384], "bfloat16"),
+    "pci": ("sbuf", [128, 8], "int32"), "pc2": ("sbuf", [128, 8], "int32"), "pcf": ("sbuf", [128, 8], "float32"),
+    "col": ("sbuf", [128, 8], "float32"),
+    "uu": ("sbuf", [128, 144], "float32"), "u2": ("sbuf", [128, 128], "float32"),
+    "v24": ("sbuf", [128, 24], "float32"), "j24": ("sbuf", [128, 24], "float32"), "offe": ("sbuf", [128, 24], "uint16"),
+    "sell": ("sbuf", [128, 128], "bfloat16"), "wd": ("sbuf", [128, 144], "bfloat16"),
+    "id1": ("sbuf", [128, 128], "bfloat16"), "id64": ("sbuf", [128, 128], "bfloat16"),
+    "id1k": ("sbuf", [128, 128], "bfloat16"), "id8k": ("sbuf", [128, 128], "bfloat16"),
+    "m32": ("sbuf", [128, 32], "float32"), "m128": ("sbuf", [128, 128], "float32"),
+    "c64": ("sbuf", [128, S], "bfloat16"), "cum": ("sbuf", [128, S], "bfloat16"),
+    "junka": ("sbuf", [128, 2 * S], "bfloat16"), "junkv": ("sbuf", [128, S], "bfloat16"),
+    "cnt": ("sbuf", [128, 8], "float32"), "offs": ("sbuf", [128, 8], "uint16"), "gsa": ("sbuf", [128, 64], "float32"),
+    "live0": ("sbuf", [128, S], "bfloat16"), "live1": ("sbuf", [128, S], "bfloat16"), "surv": ("sbuf", [128, S], "bfloat16"),
+    "k32": ("sbuf", [128, 32], "float32"), "k32t": ("sbuf", [128, 32], "float32"), "kb": ("sbuf", [128, 128], "float32"),
+    "mn": ("sbuf", [128, 8], "float32"), "win0": ("sbuf", [128, 128], "bfloat16"), "win1": ("sbuf", [128, 128], "bfloat16"),
+    "ycs": ("sbuf", [128, 8], "float32"), "own2": ("sbuf", [128, 8], "float32"), "yas": ("sbuf", [128, S], "float32"),
+    "y0": ("psum", [128, 512], "float32"), "y1": ("psum", [128, 512], "float32"), "y2": ("psum", [128, 512], "float32"),
+    "z": ("psum", [128, 512], "float32"), "s0": ("psum", [128, 512], "float32"), "s1": ("psum", [128, 512], "float32"),
+    "pf0": ("psum", [128, 512], "float32"), "pf1": ("psum", [128, 512], "float32"),
+}
+for _j in range(2):
+    SCRATCH["axb%d" % _j] = ("sbuf", [128, 384], "float16")
+    SCRATCH["ga%d" % _j] = ("sbuf", [128, 3 * S], "bfloat16")
+    SCRATCH["gb%d" % _j] = ("sbuf", [128, 3 * S], "bfloat16")
+    SCRATCH["f3%d" % _j] = ("sbuf", [128, 3 * S], "bfloat16")
+    SCRATCH["off%d" % _j] = ("sbuf", [128, S], "uint16")
+    SCRATCH["gg%d" % _j] = ("sbuf", [128, 16 * XA], "bfloat16")
+    SCRATCH["pa%d" % _j] = ("sbuf", [128, 16 * XA], "bfloat16")
+    SCRATCH["pd%d" % _j] = ("sbuf", [128, 16 * XD], "bfloat16")
+    SCRATCH["nh%d" % _j] = ("sbuf", [128, S], "bfloat16")
+for _t in range(RO):
+    SCRATCH["tt%d" % _t] = ("sbuf", [128, TW], "float32")
+    SCRATCH["rt%d" % _t] = ("sbuf", [128, TW], "float32")
+    SCRATCH["so%d" % _t] = ("sbuf", [128, 8], "float32")
+    SCRATCH["sf%d" % _t] = ("sbuf", [128, 8], "float32")
+    SCRATCH["ra%d" % _t] = ("sbuf", [128, 8], "float32")
+    SCRATCH["rb%d" % _t] = ("sbuf", [128, 8], "float32")
+
+SEMAPHORES = ["v", "a", "p", "g", "sent", "d_lv", "d_pos", "d_pf", "d_th", "d_rf", "d_out"]
+for _t in range(RO):
+    SEMAPHORES += ["rt%d" % _t, "ra%d" % _t, "rb%d" % _t]
+
+
+def bits(m):
+    return bin(m).count("1")
+
+
+def relay_of(src, dsts, T, topo):
+    ok = [c for c in topo.cores_of(src) if T.rank_of(c) is None and all(topo.may_write(c, d) for d in dsts)]
+    near = [c for c in ok if topo.die(c) == topo.die(src)]
+    return (near or ok)[0]
+
+
+def routes(rank, T, topo):
+    n = len(T.cores)
+    src = T.cores[rank]
+    msgs = []
+    for t in range(RO):
+        nxt, prv = T.cores[(rank + t + 1) % n], T.cores[(rank - t - 1) % n]
+        msgs += [("tt%d" % t, "rt%d" % t, TW, nxt), ("so%d" % t, "ra%d" % t, 1, nxt), ("sf%d" % t, "rb%d" % t, 1, prv)]
+    barred = [m[3] for m in msgs if not topo.may_write(src, m[3])]
+    via = relay_of(src, barred, T, topo) if barred else None
+    return [m + ((None if topo.may_write(src, m[3]) else via),) for m in msgs]
+
+
+def remote(g, T, topo, src, dst, out_name, in_name, cols):
+    rid, pid = topo.addr(dst, src)
+    m = topo.mask(src, dst)
+    g.remote_dma(T[out_name][:, 0:cols], T[in_name][:, 0:cols], T.sem[out_name], T.sem.sent, pid, rid, m)
+    return bits(m)
+
+
+def relay_program(g, core, T, topo):
+    total = 0
+    for r in range(len(T.cores)):
+        for (_, far, cols, dst, via) in routes(r, T, topo):
+            if via == core:
+                g.wait_ge(T.sem[far], bits(topo.mask(T.cores[r], core)))
+                total += remote(g, T, topo, core, dst, far, far, cols)
+    if total:
+        g.wait_ge(T.sem.sent, total)
+
+
+def emit(ops, queues, T):
+    writer, readers, deps = {}, {}, []
+    for i, (q, fn, rd, wr, ext) in enumerate(ops):
+        d = set()
+        for k in rd:
+            if k in writer and not (q == "p" and ops[writer[k]][0] == "p"):
+                d.add(writer[k])
+            if k[0] == "@":
+                d.update(j for j in readers.get(k, []) if ops[j][0] != q)
+        for k in wr:
+            if k in writer and not (q == "p" and ops[writer[k]][0] == "p"):
+                d.add(writer[k])
+            d.update(readers.get(k, []))
+        for k in rd:
+            readers.setdefault(k, []).append(i)
+        for k in wr:
+            writer[k] = i
+            readers[k] = []
+        d.discard(i)
+        deps.append(d)
+    need = []
+    for i, d in enumerate(deps):
+        last = {}
+        for j in d:
+            last[ops[j][0]] = max(last.get(ops[j][0], -1), j)
+        need.append(last)
+    known, snap, marked = {}, [], set()
+    for i, last in enumerate(need):
+        kq = known.setdefault(ops[i][0], {})
+        for e, j in sorted(last.items(), key=lambda x: -x[1]):
+            if kq.get(e, -1) >= j:
+                del last[e]
+            else:
+                marked.add(j)
+                kq[e] = j
+                for e2, j2 in snap[j].items():
+                    kq[e2] = max(kq.get(e2, -1), j2)
+        snap.append(dict(kq))
+    count, number, extseen = {}, {}, set()
+    for i, (q, fn, rd, wr, ext) in enumerate(ops):
+        for (name, val) in ext:
+            if (q, name) not in extseen:
+                extseen.add((q, name))
+                queues[q].wait_ge(T.sem[name], val)
+        for e, j in need[i].items():
+            queues[q].wait_ge(T.sem[e], number[j])
+        ins = fn()
+        if i in marked:
+            count[q] = count.get(q, 0) + 1
+            number[i] = count[q]
+            ins.then_inc(T.sem[q], 1)
+
+
+def rank_program(g, core, T, topo):
+    rank = T.rank_of(core)
+    if rank is None:
+        relay_program(g, core, T, topo)
+        return
+    n = len(T.cores)
+    V, A, P = g.vector, g.scalar, g.tensor
+    ops = []
+    arrive = {}
+    for r in range(n):
+        for (_, far, cols, dst, via) in routes(r, T, topo):
+            if dst == core:
+                arrive[far] = bits(topo.mask(T.cores[r] if via is None else via, core))
+    mine = {m[0]: m for m in routes(rank, T, topo)}
+    sent = [0]
+
+    def op(q, fn, rd=(), wr=(), ext=()):
+        ops.append((q, fn, list(rd), list(wr), list(ext)))
+
+    def ts(out, in0, s1, s2, op0, op1, rd, wr, ext=()):
+        if op1 is None:
+            op("v", lambda: V.tensor_scalar(out, in0, s1, None, op0), rd, wr, ext)
+        else:
+            op("v", lambda: V.tensor_scalar(out, in0, s1, s2, op0, op1), rd, wr, ext)
+
+    def tt(out, a, b, o, rd, wr, ext=()):
+        op("v", lambda: V.tensor_tensor(out, a, b, o), rd, wr, ext)
+
+    def cp(out, a, rd, wr, ext=()):
+        op("v", lambda: V.tensor_copy(out, a), rd, wr, ext)
+
+    def ms(out, c, wr):
+        op("v", lambda: V.memset(out, c), [], wr)
+
+    def act(out, a, f, rd, wr, ext=(), **kw):
+        op("a", lambda: A.activation(out, a, f, **kw), rd, wr, ext)
+
+    def mm(out, l, r, st, sp, rd, wr, ext=()):
+        op("p", lambda: P.matmul(out, l, r, st, sp), rd, wr, ext)
+
+    def iota(out, pat, base, cm, wr, f=True):
+        if f:
+            op("g", lambda: g.iota(out, pat, base, cm, allow_small_or_imprecise_dtypes=True), [], wr)
+        else:
+            op("g", lambda: g.iota(out, pat, base, cm), [], wr)
+
+    def send(name):
+        _, far, cols, dst, via = mine[name]
+
+        def fn():
+            sent[0] += remote(g, T, topo, core, dst if via is None else via, far, name, cols)
+        op("g", fn, [name], [])
+
+    Y = [T.y0, T.y1, T.y2]
+    YK = ["@y0", "@y1", "@y2"]
+    SB = [T.s0, T.s1]
+    PF = [T.pf0, T.pf1]
+    CID = [(T.id64, "id64"), (T.id1k, "id1k"), (T.id8k, "id8k")]
+
+    g.sync.dma_start(T.lvi[0:8, :], T.lv[:]).then_inc(T.sem.d_lv, 16)
+    g.scalar.dma_start(T.posb[0:24, :], T.pos[:]).then_inc(T.sem.d_pos, 16)
+    g.sync.dma_start(T.pfb[:], T.pf[:]).then_inc(T.sem.d_pf, 16)
+    g.sync.dma_start(T.thi[:, 0:1], T.th[:]).then_inc(T.sem.d_th, 16)
+    g.sync.dma_start(T.rfb[:], T.rf[:]).then_inc(T.sem.d_rf, 16)
+    LV, POS, PFD, TH, RF = [("d_lv", 16)], [("d_pos", 16)], [("d_pf", 16)], [("d_th", 16)], [("d_rf", 16)]
+
+    iota(T.pci[:, 0:1], [[0, 1]], 0, 1, ["pci"], False)
+    iota(T.u2[:], [[16, 8], [0, 16]], 0, 0, ["u2"])
+    iota(T.qp[0:24, :], [[0, 2], [-1, 3], [-3, 8]], 0, 1, ["qp"])
+    iota(T.qm[0:24, :], [[0, 2], [1, 3], [-3, 8]], -2, 1, ["qm"])
+    iota(T.uu[:], [[1, 144]], 0, 0, ["uu"])
+    iota(T.v24[:], [[0, 3], [16, 8]], 0, 0, ["v24"])
+    iota(T.j24[:], [[16, 3], [0, 8]], -48, 1, ["j24"])
+    ms(T.sel[0:32, :], 0.0, ["sel"])
+    ms(T.c64[:], 64.0, ["c64"])
+    ms(T.wa[:, S:400], 0.0, ["wa0"])
+    ms(T.wb[:, S:400], 0.0, ["wb0"])
+    for t in range(RO):
+        ms(T["tt%d" % t][:, 48:TW], 0.0, ["ttz%d" % t])
+    cp(T.pcf[:, 0:1], T.pci[:, 0:1], ["pci"], ["pcf0"])
+    ts(T.pc2[:, 0:1], T.pci[:, 0:1], 112, None, ALU.bitwise_and, None, ["pci"], ["pc20"])
+    ts(T.pc2[:, 1:2], T.pci[:, 0:1], 16, None, ALU.bitwise_and, None, ["pci"], ["pc21"])
+    ts(T.pc2[:, 2:3], T.pci[:, 0:1], 15, None, ALU.bitwise_and, None, ["pci"], ["pc22"])
+    ts(T.sell[0:8, :], T.u2[0:8, :], 1.0 / 16, T.pcf[0:8, 0:1], ALU.mult, ALU.is_equal, ["u2", "pcf0"], ["sell"])
+    for c in range(3):
+        ts(T.sel[0:24, c::16], T.qp[0:24, 8 * c:8 * c + 24], 0.0, None, ALU.is_equal, None, ["qp", "sel"], ["sel%d" % c])
+        ts(T.sel[0:24, 3 + c::16], T.qm[0:24, 16 - 8 * c:40 - 8 * c], 0.0, -1.0, ALU.is_equal, ALU.mult, ["qm", "sel"], ["sel%d" % (3 + c)])
+    cp(T.pcf[:, 1:4], T.pc2[:, 0:3], ["pc20", "pc21", "pc22"], ["pcf"])
+    G16, H16, M = T.pcf[:, 1:2], T.pcf[:, 2:3], T.pcf[:, 3:4]
+    ts(T.id1[:], T.uu[:, 0:128], T.pcf[:, 0:1], None, ALU.is_equal, None, ["uu", "pcf0"], ["id1"])
+    ts(T.col[:, 0:1], M, 3.0, 0.5, ALU.mult, ALU.add, ["pcf"], ["col0"])
+    ts(T.col[:, 1:2], M, 3.0, 1.5, ALU.mult, ALU.add, ["pcf"], ["col1"])
+    ts(T.col[:, 2:3], M, 3.0, 2.5, ALU.mult, ALU.add, ["pcf"], ["col2"])
+    cp(T.lvb[0:8, :], T.lvi[0:8, :], [], ["lvb"], LV)
+    SELK = ["sel%d" % r for r in range(6)]
+    mm(T.z[:, 0:S], T.sell[0:8, :], T.lvb[0:8, :], True, True, ["sell", "lvb"], ["@z"])
+    for i in range(3):
+        mm(Y[i][:, 0:S], T.sel[0:24, 128 * i:128 * i + 128], T.posb[0:24, :], True, True, SELK, [YK[i]], POS)
+    act(T.wa[:, 0:S], T.y0[:, 0:S], AF.Copy, ["@y0"], ["wa"])
+    act(T.wb[:, 0:S], T.y1[:, 0:S], AF.Copy, ["@y1"], ["wb"])
+    for b, (x0, x1) in enumerate(CH):
+        for i in range(4):
+            mm(PF[b][:, i:4 * (x1 - x0):4], T.id1[:], T.pfb[:, x0:x1], True, True, ["id1"], ["@pf%d" % b], PFD)
+    ts(T.v24[:], T.v24[:], G16, None, ALU.is_equal, None, ["v24", "pcf"], ["v24"])
+    ts(T.j24[:], T.j24[:], G16, None, ALU.subtract, None, ["j24", "pcf"], ["j24"])
+
+    def more_constants():
+        tt(T.j24[:], T.j24[:], T.v24[:], ALU.mult, ["j24", "v24"], ["j24"])
+        cp(T.posr[:], T.y2[:, 0:S], ["@y2"], ["posr"])
+        ts(T.offe[:], T.j24[:], 48.0, None, ALU.add, None, ["j24"], ["offe"])
+
+    def late_constants():
+        for j in range(3):
+            ts(CID[j][0][:], T.id1[:], BIG / COEF[j], None, ALU.mult, None, ["id1"], [CID[j][1]])
+        ts(T.wd[:], T.uu[:], G16, 15.0, ALU.subtract, ALU.is_equal, ["uu", "pcf"], ["wd"])
+        cp(T.thf[:, 0:1], T.thi[:, 0:1], [], ["thf"], TH)
+        ts(T.col[:, 3:4], M, 1.0 / 32, None, ALU.mult, None, ["pcf"], ["col3"])
+        ts(T.m32[:], T.u2[:, 0:32], H16, 4096.0, ALU.not_equal, ALU.mult, ["u2", "pcf"], ["m32"])
+        ts(T.m128[:], T.u2[:], G16, 4096.0, ALU.not_equal, ALU.mult, ["u2", "pcf"], ["m128"])
+        ts(T.thc[:, 0:1], T.thf[:, 0:1], BIG - 0.5, None, ALU.add, None, ["thf"], ["thc"])
+        ts(T.m32[:], T.m32[:], T.col[:, 3:4], None, ALU.add, None, ["m32", "col3"], ["m32"])
+        ts(T.m128[:], T.m128[:], T.col[:, 3:4], None, ALU.add, None, ["m128", "col3"], ["m128"])
+
+    def pfx_pool(ms_):
+        for m in ms_:
+            op("g", lambda m=m: g.affine_select(T.pfx[:, m::16], T.pfb[:, XA:S], [[0, XD]], ALU.is_gt, 0.0, 1, 0), [], ["pfx%d" % m], PFD)
+
+    def lattices(t):
+        live = "live%d" % t
+        op("v", lambda: V.tensor_tensor_scan(T.cum[:], T.z[:, 0:S], T.c64[:], 0.0, ALU.add, ALU.min), ["@z", "c64"], ["cum"])
+        for r in range(2):
+            act(T.junka[:, S * r:S * r + S], T.cum[:], AF.Sign, ["cum", "col%d" % r], ["cnt%d" % r, "junka%d" % r], bias=T.col[:, r:r + 1], scale=-1.0, accum_out=T.cnt[:, r:r + 1])
+        ts(T.junkv[:], T.cum[:], T.col[:, 2:3], None, ALU.is_lt, None, ["cum", "col2"], ["junkv"])
+        op("v", lambda: V.tensor_reduce(T.cnt[:, 2:3], T.junkv[:], AX.X, ALU.add), ["junkv"], ["cnt2"])
+        act(T[live][:], T.z[:, 0:S], AF.Copy, ["@z"], [live])
+        if t == 0:
+            more_constants()
+        cp(T.offs[:, 2:3], T.cnt[:, 2:3], ["cnt2"], ["offs2"])
+        ts(T.offs[:, 0:2], T.cnt[:, 0:2], 0.5, S / 2.0, ALU.mult, ALU.add, ["cnt0", "cnt1"], ["offs0"])
+        ts(T.offs[:, 3:5], T.cnt[:, 0:2], 0.5, S / 2.0, ALU.mult, ALU.add, ["cnt0", "cnt1"], ["offs3"])
+        cp(T.gsa[:], T.wa[:, 0:400].indirect(T.offs[:, 0:4]), ["wa", "wa0", "offs0", "offs2", "offs3"], ["gsa"])
+        tt(T["tt%d" % t][:, 0:48], T.wb[:, 0:400].indirect(T.offs[:, 2:5]), T.gsa[:, 16:64], ALU.mult,
+           ["wb", "wb0", "offs2", "offs3", "gsa", "ttz%d" % t], ["tt%d" % t])
+
+    def spread(J, src, j, ext=()):
+        cp(T["axb%d" % J][:, 128 * j:128 * j + 128], T[src][:, 0:TW].indirect(T.offe[:, 8 * j:8 * j + 8]), [src, "offe"], ["axb%d%d" % (J, j)], ext)
+
+    def dots(J, j):
+        mm(Y[j][:, 0:S], T["axb%d" % J][:, 128 * j:128 * j + 128], T.posr[:], True, True, ["axb%d%d" % (J, j), "posr"], [YK[j]])
+
+    def floor_a(J, j, on):
+        out, sc, bi = T["ga%d" % J][:, S * j:S * j + S], COEF[j] / 2048, COEF[j] * (192 - 511.5 / 2048)
+        if on == "a":
+            act(out, Y[j][:, 0:S], AF.Copy, [YK[j]], ["ga%d%d" % (J, j)], bias=bi, scale=sc)
+        else:
+            ts(out, Y[j][:, 0:S], sc, bi, ALU.mult, ALU.add, [YK[j]], ["ga%d%d" % (J, j)])
+
+    def floor_b(J, j):
+        act(T["gb%d" % J][:, S * j:S * j + S], Y[j][:, 0:S], AF.Copy, [YK[j]], ["gb%d%d" % (J, j)],
+            bias=-COEF[j] * (192 + 512.5 / 2048), scale=-COEF[j] / 2048)
+
+    def wrap(J, j):
+        c = COEF[j] * (192 - MOD[j] * (192 - (MOD[j] - 1) / (2 * MOD[j])))
+        ts(T["f3%d" % J][:, S * j:S * j + S], T["ga%d" % J][:, S * j:S * j + S], -1.0, c, ALU.mult, ALU.add, ["ga%d%d" % (J, j)], ["f3%d%d" % (J, j)])
+
+    def place_term(J, kind, j, st, sp):
+        mm(T.z[:, 0:S], T.id1[:], T["%s%d" % (kind, J)][:, S * j:S * j + S], st, sp, ["id1", "%s%d%d" % (kind, J, j)], ["@z"])
+
+    def places(J):
+        c = sum(192 * COEF[j] * (MOD[j] - 1) for j in range(3))
+        ts(T["off%d" % J][:], T.z[:, 0:S], c, None, ALU.add, None, ["@z"], ["off%d" % J])
+
+    def score_start(J, t):
+        mm(SB[J][:, 0:S], T.id8k[:], T["live%d" % t][:], True, False, ["id8k", "live%d" % t], ["@s%d" % J])
+        for kind in ("ga", "gb"):
+            for j in range(3):
+                mm(SB[J][:, 0:S], CID[j][0][:], T["%s%d" % (kind, J)][:, S * j:S * j + S], False, False,
+                   [CID[j][1], "%s%d%d" % (kind, J, j)], ["@s%d" % J])
+
+    def gather_a(J, b):
+        x0, x1 = CH[b]
+        act(T["gg%d" % J][:, 16 * x0:16 * x1], T.rfb[:].indirect(T["off%d" % J][:, x0:x1]), AF.Copy, ["off%d" % J], ["gg%d%d" % (J, b)], RF)
+
+    def gather_v(J):
+        tt(T["pd%d" % J][:], T.rfb[:].indirect(T["off%d" % J][:, XA:S]), T.pfx[:], ALU.mult,
+           ["off%d" % J] + ["pfx%d" % m for m in range(16)], ["pd%d" % J], RF)
+
+    def sum_v(J):
+        for m in range(16):
+            mm(SB[J][:, XA:S], T.wd[:, 15 - m:143 - m], T["pd%d" % J][:, m::16], False, False, ["wd", "pd%d" % J], ["@s%d" % J])
+
+    def times(J, b, r):
+        x0, x1 = CH[b]
+        w = 4 * (x1 - x0)
+        o = 16 * x0 + r * w
+        tt(T["pa%d" % J][:, o:o + w], T["gg%d" % J][:, 16 * x0 + r:16 * x1:4], PF[b][:, 0:w], ALU.mult,
+           ["gg%d%d" % (J, b), "@pf%d" % b], ["pa%d%d%d" % (J, b, r)])
+
+    def sum_a(J, b, r, last=False):
+        x0, x1 = CH[b]
+        w = 4 * (x1 - x0)
+        o = 16 * x0 + r * w
+        for i in range(4):
+            m = r + 4 * i
+            mm(SB[J][:, x0:x1], T.wd[:, 15 - m:143 - m], T["pa%d" % J][:, o + i:o + w:4], False, last and i == 3,
+               ["wd", "pa%d%d%d" % (J, b, r)], ["@s%d" % J])
+
+    def verdict(J, t):
+        name = ("so%d", "sf%d")[J] % t
+        act(T["nh%d" % J][:], SB[J][:, 0:S], AF.Sign, ["@s%d" % J, "thc"], ["nh%d" % J, name],
+            bias=T.thc[:, 0:1], scale=-1.0, accum_out=T[name][:, 0:1])
+        send(name)
+
+    def winner(J, here, far):
+        ext = [(far, arrive[far])]
+        a, b = T[here][:, 0:1], T[far][:, 0:1]
+        ts(T.k32[:], T.m32[:], a, b, ALU.add, ALU.add, ["m32", here], ["k32"], ext)
+        ts(T.kb[:], T.m128[:], a, b, ALU.add, ALU.add, ["m128", here], ["kb"])
+        op("v", lambda: V.transpose(T.k32t[:], T.k32[:]), ["k32"], ["k32t"])
+        op("v", lambda: V.tensor_reduce(T.mn[:, 0:1], T.k32t[:], AX.X, ALU.min), ["k32t"], ["mn"])
+        ts(T["win%d" % J][:], T.kb[:], T.mn[:, 0:1], None, ALU.is_le, None, ["kb", "mn"], ["win%d" % J])
+
+    pfx_pool(range(POOL_PRE))
+    for t in range(RO):
+        live = "live%d" % t
+        lattices(t)
+        send("tt%d" % t)
+        if t == 0:
+            pfx_pool(range(POOL_PRE, POOL_PRE + POOL_POST))
+            for m in range(POOL_PRE + POOL_POST, 16):
+                act(T.pfx[:, m::16], T.pfb[:, XA:S], AF.Copy, [], ["pfx%d" % m], PFD)
+        for j in range(3):
+            spread(0, "tt%d" % t, j)
+            dots(0, j)
+        floor_a(0, 0, "a")
+        floor_a(0, 1, "a")
+        floor_a(0, 2, "v")
+        wrap(0, 0)
+        wrap(0, 2)
+        wrap(0, 1)
+        for i, (kind, j) in enumerate([("ga", 0), ("ga", 2), ("ga", 1), ("f3", 0), ("f3", 2), ("f3", 1)]):
+            place_term(0, kind, j, i == 0, i == 5)
+        for j in range(3):
+            floor_b(0, j)
+        if t == 0:
+            late_constants()
+        places(0)
+        gather_a(0, 0)
+        gather_v(0)
+        score_start(0, t)
+        gather_a(0, 1)
+        sum_v(0)
+        for j in range(3):
+            spread(1, "rt%d" % t, j, [("rt%d" % t, arrive["rt%d" % t])])
+            dots(1, j)
+        for r in range(4):
+            times(0, 0, r)
+            sum_a(0, 0, r)
+        for j in range(3):
+            floor_a(1, j, "a")
+        for r in range(2):
+            times(0, 1, r)
+            sum_a(0, 1, r)
+        for j in range(3):
+            place_term(1, "ga", j, j == 0, False)
+        for j in range(3):
+            wrap(1, j)
+            place_term(1, "f3", j, False, j == 2)
+        for j in range(3):
+            floor_b(1, j)
+        times(0, 1, 2)
+        places(1)
+        sum_a(0, 1, 2)
+        times(0, 1, 3)
+        sum_a(0, 1, 3, True)
+        gather_a(1, 0)
+        gather_v(1)
+        score_start(1, t)
+        verdict(0, t)
+        gather_a(1, 1)
+        sum_v(1)
+        mm(T.y0[:, 0:S], T.id8k[:], T[live][:], True, False, ["id8k", live], ["@y0"])
+        mm(T.y0[:, 0:S], T.id1[:], T.nh0[:], False, False, ["id1", "nh0"], ["@y0"])
+        if t == RO - 1:
+            for u in range(RO):
+                mm(T.z[0:8, 0:S], T.id1[:, ::16], T["live%d" % u][:], u == 0, False, ["id1", "live%d" % u], ["@z"])
+        for b in range(2):
+            for r in range(4):
+                times(1, b, r)
+                sum_a(1, b, r, b == 1 and r == 3)
+        ts(T.own2[:, 0:1], T["so%d" % t][:, 0:1], -2.0 * S, None, ALU.add, None, ["so%d" % t], ["own2"])
+        verdict(1, t)
+        winner(1, "sf%d" % t, "ra%d" % t)
+        mm(T.y0[:, 0:S], T.win1[:], T.nh1[:], False, True, ["win1", "nh1"], ["@y0"])
+        ts(T.surv[:], T.y0[:, 0:S], BIG + 1.5, None, ALU.is_ge, None, ["@y0"], ["surv"])
+        winner(0, "so%d" % t, "rb%d" % t)
+        if t < RO - 1:
+            mm(T.z[:, 0:S], T.win0[:], T.surv[:], True, True, ["win0", "surv"], ["@z"])
+        else:
+            mm(T.z[0:8, 0:S], T.win0[:, ::16], T.surv[:], False, True, ["win0", "surv"], ["@z"])
+        ts(T.ycs[:, t:t + 1], T.own2[:, 0:1], T["rb%d" % t][:, 0:1], -0.5, ALU.add, ALU.mult, ["own2"], ["ycs%d" % t])
+    cp(T.yas[0:8, :], T.z[0:8, 0:S], ["@z"], ["yas"])
+    op("a", lambda: g.scalar.dma_start(T.yc[:], T.ycs[:, 0:RO]).then_inc(T.sem.d_out, 16), ["ycs%d" % t for t in range(RO)], [])
+    op("s", lambda: g.sync.dma_start(T.ya[:], T.yas[0:8, :]).then_inc(T.sem.d_out, 16), ["yas"], [])
+    emit(ops, {"v": V, "a": A, "p": P, "g": g, "s": g.sync}, T)
+    g.sync.wait_ge(T.sem.d_out, 32)
+    g.wait_ge(T.sem.sent, sent[0])

@@ -2,54 +2,58 @@ from concourse.mybir import AluOpType as ALU, AxisListType as AX, ActivationFunc
 
 S = 384
 RO = 2
-XA = 240
-XD = S - XA
-CH = [(0, 128), (128, XA)]
+XA = [192, 240]
+X0 = min(XA)
+XD = S - X0
+L1, L = 152, 64
+LATE_B = 1
 COEF = [128.0, 8.0, 1.0]
 MOD = [16.0, 16.0, 8.0]
 BIG = 8192.0
-TW = 56
-POOL_PRE, POOL_POST = 5, 6
+WB = 400
+COPIES = {"g0": 4, "g1": 2, "a0": 3, "a1": 2, "v0": 2, "v1": 3}
 
 SCRATCH = {
-    "posb": ("sbuf", [128, S], "bfloat16"), "lvi": ("sbuf", [128, S], "int32"), "lvb": ("sbuf", [128, S], "bfloat16"),
+    "posb": ("sbuf", [128, S], "bfloat16"), "tb": ("sbuf", [128, S], "bfloat16"),
+    "lvi": ("sbuf", [128, S], "int32"), "lvb": ("sbuf", [128, S], "float16"),
     "pfb": ("sbuf", [128, S], "bfloat16"), "rfb": ("sbuf", [128, 2048], "bfloat16"),
-    "thi": ("sbuf", [128, 8], "int32"), "thf": ("sbuf", [128, 8], "float32"), "thc": ("sbuf", [128, 8], "float32"),
-    "wa": ("sbuf", [128, 400], "bfloat16"), "wb": ("sbuf", [128, 400], "bfloat16"), "posr": ("sbuf", [128, S], "float16"),
+    "thi": ("sbuf", [128, 8], "int32"), "thc": ("sbuf", [128, 8], "float32"),
+    "w": ("sbuf", [128, 2 * WB], "bfloat16"), "posr": ("sbuf", [128, S], "bfloat16"),
     "pfx": ("sbuf", [128, 16 * XD], "bfloat16"),
-    "qp": ("sbuf", [128, 48], "float32"), "qm": ("sbuf", [128, 48], "float32"), "sel": ("sbuf", [128, 384], "bfloat16"),
-    "pci": ("sbuf", [128, 8], "int32"), "pc2": ("sbuf", [128, 8], "int32"), "pcf": ("sbuf", [128, 8], "float32"),
-    "col": ("sbuf", [128, 8], "float32"),
-    "uu": ("sbuf", [128, 144], "float32"), "u2": ("sbuf", [128, 128], "float32"),
-    "v24": ("sbuf", [128, 24], "float32"), "j24": ("sbuf", [128, 24], "float32"), "offe": ("sbuf", [128, 24], "uint16"),
-    "sell": ("sbuf", [128, 128], "bfloat16"), "wd": ("sbuf", [128, 144], "bfloat16"),
+    "qp": ("sbuf", [128, 96], "bfloat16"), "qm": ("sbuf", [128, 96], "bfloat16"), "sel": ("sbuf", [128, 384], "bfloat16"),
+    "sgn": ("sbuf", [128, 128], "bfloat16"), "sb1": ("sbuf", [128, 128], "bfloat16"), "sb2": ("sbuf", [128, 128], "bfloat16"),
+    "pci": ("sbuf", [128, 8], "int32"), "pc2": ("sbuf", [128, 8], "int32"), "sb3": ("sbuf", [128, 128], "bfloat16"),
+    "col": ("sbuf", [128, 8], "float32"), "k2": ("sbuf", [128, 8], "float32"), "blk": ("sbuf", [128, 16], "bfloat16"),
+    "uu": ("sbuf", [128, 128], "bfloat16"), "u2": ("sbuf", [128, 128], "bfloat16"), "zero": ("sbuf", [128, 128], "bfloat16"),
+    "pen1": ("sbuf", [128, 128], "bfloat16"),
+    "offe": ("sbuf", [128, 8], "uint16"), "thr": ("sbuf", [128, 128], "bfloat16"),
+    "cst": ("sbuf", [128, S], "bfloat16"), "ramp": ("sbuf", [128, S], "float16"),
+    "sell": ("sbuf", [128, 128], "float16"), "wd": ("sbuf", [128, 144], "bfloat16"),
     "id1": ("sbuf", [128, 128], "bfloat16"), "id64": ("sbuf", [128, 128], "bfloat16"),
     "id1k": ("sbuf", [128, 128], "bfloat16"), "id8k": ("sbuf", [128, 128], "bfloat16"),
-    "m32": ("sbuf", [128, 32], "float32"), "m128": ("sbuf", [128, 128], "float32"),
-    "c64": ("sbuf", [128, S], "bfloat16"), "cum": ("sbuf", [128, S], "bfloat16"),
-    "junka": ("sbuf", [128, 2 * S], "bfloat16"), "junkv": ("sbuf", [128, S], "bfloat16"),
-    "cnt": ("sbuf", [128, 8], "float32"), "offs": ("sbuf", [128, 8], "uint16"), "gsa": ("sbuf", [128, 64], "float32"),
-    "live0": ("sbuf", [128, S], "bfloat16"), "live1": ("sbuf", [128, S], "bfloat16"), "surv": ("sbuf", [128, S], "bfloat16"),
-    "k32": ("sbuf", [128, 32], "float32"), "k32t": ("sbuf", [128, 32], "float32"), "kb": ("sbuf", [128, 128], "float32"),
-    "mn": ("sbuf", [128, 8], "float32"), "win0": ("sbuf", [128, 128], "bfloat16"), "win1": ("sbuf", [128, 128], "bfloat16"),
-    "ycs": ("sbuf", [128, 8], "float32"), "own2": ("sbuf", [128, 8], "float32"), "yas": ("sbuf", [128, S], "float32"),
+    "pen32": ("sbuf", [128, 32], "bfloat16"), "pen": ("sbuf", [128, 128], "bfloat16"),
+    "cum": ("sbuf", [128, S], "float16"), "junk": ("sbuf", [128, S], "bfloat16"), "sc": ("sbuf", [128, 2 * S], "float16"),
+    "cnt": ("sbuf", [128, 8], "float32"), "offs": ("sbuf", [128, 8], "uint16"), "gs": ("sbuf", [128, 96], "bfloat16"),
+    "live0": ("sbuf", [128, S], "bfloat16"), "live1": ("sbuf", [128, S], "bfloat16"), "surv": ("sbuf", [128, S], "float16"),
+    "k32": ("sbuf", [128, 32], "float32"), "k32t": ("sbuf", [128, 32], "float32"),
+    "mn": ("sbuf", [128, 8], "float32"), "win0": ("sbuf", [128, 128], "float16"), "win1": ("sbuf", [128, 128], "bfloat16"),
+    "ycs": ("sbuf", [128, 8], "float32"), "yas": ("sbuf", [128, S], "float32"),
     "y0": ("psum", [128, 512], "float32"), "y1": ("psum", [128, 512], "float32"), "y2": ("psum", [128, 512], "float32"),
     "z": ("psum", [128, 512], "float32"), "s0": ("psum", [128, 512], "float32"), "s1": ("psum", [128, 512], "float32"),
-    "pf0": ("psum", [128, 512], "float32"), "pf1": ("psum", [128, 512], "float32"),
+    "pf4": ("psum", [128, 1024], "float32"),
 }
 for _j in range(2):
-    SCRATCH["axb%d" % _j] = ("sbuf", [128, 384], "float16")
     SCRATCH["ga%d" % _j] = ("sbuf", [128, 3 * S], "bfloat16")
     SCRATCH["gb%d" % _j] = ("sbuf", [128, 3 * S], "bfloat16")
     SCRATCH["f3%d" % _j] = ("sbuf", [128, 3 * S], "bfloat16")
     SCRATCH["off%d" % _j] = ("sbuf", [128, S], "uint16")
-    SCRATCH["gg%d" % _j] = ("sbuf", [128, 16 * XA], "bfloat16")
-    SCRATCH["pa%d" % _j] = ("sbuf", [128, 16 * XA], "bfloat16")
-    SCRATCH["pd%d" % _j] = ("sbuf", [128, 16 * XD], "bfloat16")
+    SCRATCH["pr%d" % _j] = ("sbuf", [128, 16 * S], "bfloat16")
     SCRATCH["nh%d" % _j] = ("sbuf", [128, S], "bfloat16")
+    SCRATCH["pk%d" % _j] = ("sbuf", [128, 32], "float32")
+    SCRATCH["tot%d" % _j] = ("sbuf", [128, 8], "float32")
 for _t in range(RO):
-    SCRATCH["tt%d" % _t] = ("sbuf", [128, TW], "float32")
-    SCRATCH["rt%d" % _t] = ("sbuf", [128, TW], "float32")
+    SCRATCH["ax%d" % _t] = ("sbuf", [128, 384], "bfloat16")
+    SCRATCH["rt%d" % _t] = ("sbuf", [128, 384], "bfloat16")
     SCRATCH["so%d" % _t] = ("sbuf", [128, 8], "float32")
     SCRATCH["sf%d" % _t] = ("sbuf", [128, 8], "float32")
     SCRATCH["ra%d" % _t] = ("sbuf", [128, 8], "float32")
@@ -76,7 +80,7 @@ def routes(rank, T, topo):
     msgs = []
     for t in range(RO):
         nxt, prv = T.cores[(rank + t + 1) % n], T.cores[(rank - t - 1) % n]
-        msgs += [("tt%d" % t, "rt%d" % t, TW, nxt), ("so%d" % t, "ra%d" % t, 1, nxt), ("sf%d" % t, "rb%d" % t, 1, prv)]
+        msgs += [("ax%d" % t, "rt%d" % t, 384, nxt), ("so%d" % t, "ra%d" % t, 1, nxt), ("sf%d" % t, "rb%d" % t, 2, prv)]
     barred = [m[3] for m in msgs if not topo.may_write(src, m[3])]
     via = relay_of(src, barred, T, topo) if barred else None
     return [m + ((None if topo.may_write(src, m[3]) else via),) for m in msgs]
@@ -105,7 +109,7 @@ def emit(ops, queues, T):
     for i, (q, fn, rd, wr, ext) in enumerate(ops):
         d = set()
         for k in rd:
-            if k in writer and not (q == "p" and ops[writer[k]][0] == "p"):
+            if k in writer and (k[0] == "!" or not (q == "p" and ops[writer[k]][0] == "p")):
                 d.add(writer[k])
             if k[0] == "@":
                 d.update(j for j in readers.get(k, []) if ops[j][0] != q)
@@ -187,6 +191,9 @@ def rank_program(g, core, T, topo):
     def ms(out, c, wr):
         op("v", lambda: V.memset(out, c), [], wr)
 
+    def scan(out, d0, d1, op0, op1, rd, wr):
+        op("v", lambda: V.tensor_tensor_scan(out, d0, d1, 0.0, op0, op1), rd, wr)
+
     def act(out, a, f, rd, wr, ext=(), **kw):
         op("a", lambda: A.activation(out, a, f, **kw), rd, wr, ext)
 
@@ -199,109 +206,128 @@ def rank_program(g, core, T, topo):
         else:
             op("g", lambda: g.iota(out, pat, base, cm), [], wr)
 
-    def send(name):
+    def send(name, rd):
         _, far, cols, dst, via = mine[name]
 
         def fn():
             sent[0] += remote(g, T, topo, core, dst if via is None else via, far, name, cols)
-        op("g", fn, [name], [])
+        op("g", fn, rd, [])
+
+    def came(name):
+        return [(name, arrive[name])]
 
     Y = [T.y0, T.y1, T.y2]
     YK = ["@y0", "@y1", "@y2"]
-    SB = [T.s0, T.s1]
-    PF = [T.pf0, T.pf1]
     CID = [(T.id64, "id64"), (T.id1k, "id1k"), (T.id8k, "id8k")]
 
     g.sync.dma_start(T.lvi[0:8, :], T.lv[:]).then_inc(T.sem.d_lv, 16)
     g.scalar.dma_start(T.posb[0:24, :], T.pos[:]).then_inc(T.sem.d_pos, 16)
     g.sync.dma_start(T.pfb[:], T.pf[:]).then_inc(T.sem.d_pf, 16)
-    g.sync.dma_start(T.thi[:, 0:1], T.th[:]).then_inc(T.sem.d_th, 16)
     g.sync.dma_start(T.rfb[:], T.rf[:]).then_inc(T.sem.d_rf, 16)
+    g.scalar.dma_start(T.thi[:, 0:1], T.th[:]).then_inc(T.sem.d_th, 16)
     LV, POS, PFD, TH, RF = [("d_lv", 16)], [("d_pos", 16)], [("d_pf", 16)], [("d_th", 16)], [("d_rf", 16)]
 
-    iota(T.pci[:, 0:1], [[0, 1]], 0, 1, ["pci"], False)
-    iota(T.u2[:], [[16, 8], [0, 16]], 0, 0, ["u2"])
-    iota(T.qp[0:24, :], [[0, 2], [-1, 3], [-3, 8]], 0, 1, ["qp"])
-    iota(T.qm[0:24, :], [[0, 2], [1, 3], [-3, 8]], -2, 1, ["qm"])
-    iota(T.uu[:], [[1, 144]], 0, 0, ["uu"])
-    iota(T.v24[:], [[0, 3], [16, 8]], 0, 0, ["v24"])
-    iota(T.j24[:], [[16, 3], [0, 8]], -48, 1, ["j24"])
-    ms(T.sel[0:32, :], 0.0, ["sel"])
-    ms(T.c64[:], 64.0, ["c64"])
-    ms(T.wa[:, S:400], 0.0, ["wa0"])
-    ms(T.wb[:, S:400], 0.0, ["wb0"])
-    for t in range(RO):
-        ms(T["tt%d" % t][:, 48:TW], 0.0, ["ttz%d" % t])
-    cp(T.pcf[:, 0:1], T.pci[:, 0:1], ["pci"], ["pcf0"])
-    ts(T.pc2[:, 0:1], T.pci[:, 0:1], 112, None, ALU.bitwise_and, None, ["pci"], ["pc20"])
-    ts(T.pc2[:, 1:2], T.pci[:, 0:1], 16, None, ALU.bitwise_and, None, ["pci"], ["pc21"])
-    ts(T.pc2[:, 2:3], T.pci[:, 0:1], 15, None, ALU.bitwise_and, None, ["pci"], ["pc22"])
-    ts(T.sell[0:8, :], T.u2[0:8, :], 1.0 / 16, T.pcf[0:8, 0:1], ALU.mult, ALU.is_equal, ["u2", "pcf0"], ["sell"])
+    COUNT = [("s0", "z", "s1", "y0"), ("y0", "y2", "y1", "s1")]
+
+    def thresholds(t):
+        for bank, r in zip(COUNT[t], (0, 2, 1)):
+            mm(T[bank][:, 0:S], T.thr[32 * r:32 * r + 1, :], T.cst[32 * r:32 * r + 1, :], True, False, ["thr", "cst"], ["@" + bank, "!" + bank])
+
+    iota(T.thr[0:96, :], [[0, 8], [3072, 16]], 512, 32, ["thr"])
+    iota(T.qp[0:24, 0:48], [[-1, 3], [-3, 8], [0, 2]], 0, 1, ["qp0"])
+    iota(T.qm[0:24, 0:48], [[1, 3], [-3, 8], [0, 2]], -2, 1, ["qm0"])
+    iota(T.sgn[0:24, :], [[0, 8], [-2, 2], [0, 8]], 1, 0, ["sgn"])
+    iota(T.u2[0:8, :], [[-1, 8], [0, 16]], 0, 1, ["u2"])
+    iota(T.pci[:, 0:4], [[128, 4]], 0, 1, ["pci"], False)
+    iota(T.uu[:], [[-1, 128]], 0, 1, ["uu"])
+    ms(T.cst[:], -1.0 / 1024, ["cst"])
+    for c in (6, 7):
+        ms(T.sel[0:24, c::8], 0.0, ["sel%d" % c])
+    scan(T.ramp[:], T.cst[:], T.cst[:], ALU.add, ALU.min, ["cst"], ["ramp"])
+    thresholds(0)
+    cp(T.qp[0:24, 48:96], T.qp[0:24, 0:48], ["qp0"], ["qp1"])
     for c in range(3):
-        ts(T.sel[0:24, c::16], T.qp[0:24, 8 * c:8 * c + 24], 0.0, None, ALU.is_equal, None, ["qp", "sel"], ["sel%d" % c])
-        ts(T.sel[0:24, 3 + c::16], T.qm[0:24, 16 - 8 * c:40 - 8 * c], 0.0, -1.0, ALU.is_equal, ALU.mult, ["qm", "sel"], ["sel%d" % (3 + c)])
-    cp(T.pcf[:, 1:4], T.pc2[:, 0:3], ["pc20", "pc21", "pc22"], ["pcf"])
-    G16, H16, M = T.pcf[:, 1:2], T.pcf[:, 2:3], T.pcf[:, 3:4]
-    ts(T.id1[:], T.uu[:, 0:128], T.pcf[:, 0:1], None, ALU.is_equal, None, ["uu", "pcf0"], ["id1"])
-    ts(T.col[:, 0:1], M, 3.0, 0.5, ALU.mult, ALU.add, ["pcf"], ["col0"])
-    ts(T.col[:, 1:2], M, 3.0, 1.5, ALU.mult, ALU.add, ["pcf"], ["col1"])
-    ts(T.col[:, 2:3], M, 3.0, 2.5, ALU.mult, ALU.add, ["pcf"], ["col2"])
+        ts(T.sel[0:24, c::8], T.qp[0:24, 16 * c:16 * c + 48], 0.0, None, ALU.is_equal, None, ["qp0", "qp1"], ["sel%d" % c])
+    cp(T.qm[0:24, 48:96], T.qm[0:24, 0:48], ["qm0"], ["qm1"])
+    for c in range(3):
+        ts(T.sel[0:24, 3 + c:256:8], T.qm[0:24, 32 - 16 * c:64 - 16 * c], 0.0, None, ALU.is_equal, None, ["qm0", "qm1"], ["sel%d" % (3 + c)])
+    for c in range(3):
+        ts(T.sel[0:24, 259 + c::8], T.qm[0:24, 64 - 16 * c:80 - 16 * c], 0.0, -1.0, ALU.is_equal, ALU.mult, ["qm0", "qm1"], ["selr%d" % c])
+    SELK = ["sel%d" % r for r in range(8)]
+    tt(T.sb2[0:24, :], T.sel[0:24, 128:256], T.sgn[0:24, :], ALU.mult, SELK + ["sgn"], ["sb2"])
+    ts(T.sb1[0:24, :], T.sb2[0:24, :], -1.0, 0.0, ALU.mult, ALU.max, ["sb2"], ["sb1"])
     cp(T.lvb[0:8, :], T.lvi[0:8, :], [], ["lvb"], LV)
-    SELK = ["sel%d" % r for r in range(6)]
-    mm(T.z[:, 0:S], T.sell[0:8, :], T.lvb[0:8, :], True, True, ["sell", "lvb"], ["@z"])
-    for i in range(3):
-        mm(Y[i][:, 0:S], T.sel[0:24, 128 * i:128 * i + 128], T.posb[0:24, :], True, True, SELK, [YK[i]], POS)
-    act(T.wa[:, 0:S], T.y0[:, 0:S], AF.Copy, ["@y0"], ["wa"])
-    act(T.wb[:, 0:S], T.y1[:, 0:S], AF.Copy, ["@y1"], ["wb"])
-    for b, (x0, x1) in enumerate(CH):
-        for i in range(4):
-            mm(PF[b][:, i:4 * (x1 - x0):4], T.id1[:], T.pfb[:, x0:x1], True, True, ["id1"], ["@pf%d" % b], PFD)
-    ts(T.v24[:], T.v24[:], G16, None, ALU.is_equal, None, ["v24", "pcf"], ["v24"])
-    ts(T.j24[:], T.j24[:], G16, None, ALU.subtract, None, ["j24", "pcf"], ["j24"])
+    ts(T.sell[0:8, :], T.u2[0:8, :], 0.0, None, ALU.is_equal, None, ["u2"], ["sell"])
+    scan(T.cum[0:8, :], T.lvb[0:8, :], T.lvb[0:8, :], ALU.add, ALU.max, ["lvb"], ["cum"])
+    act(T.ax0[:], T.cst[:], AF.Copy, ["cst"], ["ax0"], scale=0.0)
+    for i in range(2):
+        act(T.k2[:, i:i + 1], T.cst[:, 0:1], AF.Copy, ["cst"], ["k2%d" % i], scale=0.0, bias=float(S + 2 * WB * i))
+        act(T.w[:, WB * i + S:WB * i + WB], T.cst[:, 0:WB - S], AF.Copy, ["cst"], ["wz%d" % i], scale=0.0)
+    act(T.sb3[0:1, :], T.sgn[0:1, :], AF.Copy, ["sgn"], ["sb3"], scale=1536.0 * 1024)
+    act(T.tb[0:24, :], T.posb[0:24, :], AF.Copy, [], ["tb"], POS, bias=1536.0)
+    mm(T.y0[:, 0:S], T.sel[0:24, 0:128], T.posb[0:24, :], True, True, SELK, ["@y0"], POS)
+    mm(T.y1[:, 0:S], T.sb3[0:1, :], T.cst[0:1, :], True, False, ["sb3", "cst"], ["@y1"])
+    mm(T.y1[:, 0:S], T.sb1[0:24, :], T.posb[0:24, :], False, False, ["sb1"], ["@y1"])
+    mm(T.y1[:, 0:S], T.sb2[0:24, :], T.tb[0:24, :], False, True, ["sb2", "tb"], ["@y1"])
+    act(T.w[:, 0:S], T.y0[:, 0:S], AF.Copy, ["@y0"], ["wa"])
+    act(T.w[:, WB:WB + S], T.y1[:, 0:S], AF.Copy, ["@y1"], ["wb"])
 
-    def more_constants():
-        tt(T.j24[:], T.j24[:], T.v24[:], ALU.mult, ["j24", "v24"], ["j24"])
-        cp(T.posr[:], T.y2[:, 0:S], ["@y2"], ["posr"])
-        ts(T.offe[:], T.j24[:], 48.0, None, ALU.add, None, ["j24"], ["offe"])
+    todo = list(range(16))
 
-    def late_constants():
+    def pfx_copies(who):
+        for _ in range(COPIES[who]):
+            m = todo.pop()
+            out, src = T.pfx[:, m::16], T.pfb[:, X0:S]
+            if who[0] == "g":
+                op("g", lambda out=out: g.affine_select(out, src, [[0, XD]], ALU.is_gt, 0.0, 1, 0), [], ["pfx%d" % m], PFD)
+            elif who[0] == "a":
+                act(out, src, AF.Copy, [], ["pfx%d" % m], PFD)
+            else:
+                cp(out, src, [], ["pfx%d" % m], PFD)
+
+    def select(out, src, pat, cmp, fill, base, cm, rd, wr):
+        op("g", lambda: g.affine_select(out, src, pat, cmp, fill, base, cm), rd, wr)
+
+    def pool_constants():
+        iota(T.zero[:], [[0, 128]], 0, 0, ["zero"])
         for j in range(3):
-            ts(CID[j][0][:], T.id1[:], BIG / COEF[j], None, ALU.mult, None, ["id1"], [CID[j][1]])
-        ts(T.wd[:], T.uu[:], G16, 15.0, ALU.subtract, ALU.is_equal, ["uu", "pcf"], ["wd"])
-        cp(T.thf[:, 0:1], T.thi[:, 0:1], [], ["thf"], TH)
-        ts(T.col[:, 3:4], M, 1.0 / 32, None, ALU.mult, None, ["pcf"], ["col3"])
-        ts(T.m32[:], T.u2[:, 0:32], H16, 4096.0, ALU.not_equal, ALU.mult, ["u2", "pcf"], ["m32"])
-        ts(T.m128[:], T.u2[:], G16, 4096.0, ALU.not_equal, ALU.mult, ["u2", "pcf"], ["m128"])
-        ts(T.thc[:, 0:1], T.thf[:, 0:1], BIG - 0.5, None, ALU.add, None, ["thf"], ["thc"])
-        ts(T.m32[:], T.m32[:], T.col[:, 3:4], None, ALU.add, None, ["m32", "col3"], ["m32"])
-        ts(T.m128[:], T.m128[:], T.col[:, 3:4], None, ALU.add, None, ["m128", "col3"], ["m128"])
+            select(CID[j][0][:], T.zero[:], [[-1, 128]], ALU.not_equal, BIG / COEF[j], 0, 1, ["zero"], [CID[j][1]])
+        iota(T.ax1[:], [[0, 384]], 0, 0, ["ax1"])
+        iota(T.wd[:], [[0, 144]], 0, 0, ["wd0"])
+        iota(T.blk[:, 0:8], [[0, 8]], 1, 0, ["blk0"])
+        select(T.blk[:, 8:16], T.blk[:, 0:8], [[-16, 8]], ALU.is_ge, 0.0, 0, 1, ["blk0"], ["blk1"])
+        select(T.wd[:, 15:143:16], T.blk[:, 8:16], [[16, 8]], ALU.is_ge, 0.0, 15, -1, ["blk1", "wd0"], ["wd"])
+        select(T.pen1[:], T.zero[:], [[-16, 8], [0, 16]], ALU.is_ge, 4096.0, 0, 1, ["zero"], ["pen1"])
+        select(T.pen[:], T.pen1[:], [[16, 8], [0, 16]], ALU.is_ge, 4096.0, 15, -1, ["pen1"], ["pen"])
+        for q in range(0, 128, 32):
+            select(T.pen32[q:q + 32, :], T.pen[q:q + 32, q:q + 32], [[0, 32]], ALU.is_gt, 0.0, 1, 0, ["pen"], ["pen32%d" % q])
 
-    def pfx_pool(ms_):
-        for m in ms_:
-            op("g", lambda m=m: g.affine_select(T.pfx[:, m::16], T.pfb[:, XA:S], [[0, XD]], ALU.is_gt, 0.0, 1, 0), [], ["pfx%d" % m], PFD)
-
-    def lattices(t):
-        live = "live%d" % t
-        op("v", lambda: V.tensor_tensor_scan(T.cum[:], T.z[:, 0:S], T.c64[:], 0.0, ALU.add, ALU.min), ["@z", "c64"], ["cum"])
-        for r in range(2):
-            act(T.junka[:, S * r:S * r + S], T.cum[:], AF.Sign, ["cum", "col%d" % r], ["cnt%d" % r, "junka%d" % r], bias=T.col[:, r:r + 1], scale=-1.0, accum_out=T.cnt[:, r:r + 1])
-        ts(T.junkv[:], T.cum[:], T.col[:, 2:3], None, ALU.is_lt, None, ["cum", "col2"], ["junkv"])
-        op("v", lambda: V.tensor_reduce(T.cnt[:, 2:3], T.junkv[:], AX.X, ALU.add), ["junkv"], ["cnt2"])
-        act(T[live][:], T.z[:, 0:S], AF.Copy, ["@z"], [live])
+    def lattices(t, pick, k, flags):
+        live, key = "live%d" % t, ("sell", "win0")[t]
+        b0, b2, b1, bl = COUNT[t]
+        for bank in (b0, b2, b1):
+            mm(T[bank][:, 0:S], pick, T.cum[0:k, :], False, True, [key, "cum", "!" + bank], ["@" + bank])
         if t == 0:
-            more_constants()
-        cp(T.offs[:, 2:3], T.cnt[:, 2:3], ["cnt2"], ["offs2"])
-        ts(T.offs[:, 0:2], T.cnt[:, 0:2], 0.5, S / 2.0, ALU.mult, ALU.add, ["cnt0", "cnt1"], ["offs0"])
-        ts(T.offs[:, 3:5], T.cnt[:, 0:2], 0.5, S / 2.0, ALU.mult, ALU.add, ["cnt0", "cnt1"], ["offs3"])
-        cp(T.gsa[:], T.wa[:, 0:400].indirect(T.offs[:, 0:4]), ["wa", "wa0", "offs0", "offs2", "offs3"], ["gsa"])
-        tt(T["tt%d" % t][:, 0:48], T.wb[:, 0:400].indirect(T.offs[:, 2:5]), T.gsa[:, 16:64], ALU.mult,
-           ["wb", "wb0", "offs2", "offs3", "gsa", "ttz%d" % t], ["tt%d" % t])
+            mm(T.y2[:, 0:S], T.sel[0:24, 256:384], T.posb[0:24, :], True, True, SELK + ["selr%d" % c for c in range(3)], ["@y2"])
+        mm(T[bl][:, 0:S], pick, T[flags][0:k, :], True, True, [key, flags], ["@" + bl])
+        scan(T.sc[:, 0:S], T[b0][:, 0:S], T.ramp[:], ALU.min, ALU.max, ["@" + b0, "ramp"], ["sc0"])
+        act(T.junk[:], T[b2][:, 0:S], AF.Sign, ["@" + b2], ["cnt", "junk"], scale=-1.0, accum_out=T.cnt[:, 0:1])
+        scan(T.sc[:, S:2 * S], T[b1][:, 0:S], T.ramp[:], ALU.min, ALU.max, ["@" + b1, "ramp"], ["sc1"])
+        ts(T.offs[:, 0:6:5], T.k2[:, 0:2], T.cnt[:, 0:1], 0.5, ALU.add, ALU.mult, ["k20", "k21", "cnt"], ["offs0"])
+        ts(T.offs[:, 1:3], T.sc[:, S - 1::S], -1024.0, None, ALU.mult, None, ["sc0", "sc1"], ["offs1"])
+        ts(T.offs[:, 3:5], T.sc[:, S - 1::S], -1024.0, float(WB), ALU.mult, ALU.add, ["sc0", "sc1"], ["offs3"])
+        if t == 0:
+            cp(T.offe[:, 0:4], T.pci[:, 0:4], ["pci"], ["offe"])
+            act(T.posr[:], T.y2[:, 0:S], AF.Copy, ["@y2"], ["posr"])
+        act(T[live][:], T[bl][:, 0:S], AF.Copy, ["@" + bl], [live])
+        cp(T.gs[:], T.w[:].indirect(T.offs[:, 0:6]), ["wa", "wb", "wz0", "wz1", "offs0", "offs1", "offs3"], ["gs"])
+        tt(T["ax%d" % t][:].indirect(T.offe[:, 0:3]), T.gs[:, 0:48], T.gs[:, 48:96], ALU.mult, ["gs", "offe"], ["ax%d" % t])
+        send("ax%d" % t, ["ax%d" % t])
 
-    def spread(J, src, j, ext=()):
-        cp(T["axb%d" % J][:, 128 * j:128 * j + 128], T[src][:, 0:TW].indirect(T.offe[:, 8 * j:8 * j + 8]), [src, "offe"], ["axb%d%d" % (J, j)], ext)
-
-    def dots(J, j):
-        mm(Y[j][:, 0:S], T["axb%d" % J][:, 128 * j:128 * j + 128], T.posr[:], True, True, ["axb%d%d" % (J, j), "posr"], [YK[j]])
+    def dots(src, rd, ext=()):
+        for j in range(3):
+            i = (j + 2) % 3
+            mm(Y[j][:, 0:S], T[src][:, 128 * i:128 * i + 128], T.posr[:], True, True, rd + ["posr"], [YK[j]], ext)
 
     def floor_a(J, j, on):
         out, sc, bi = T["ga%d" % J][:, S * j:S * j + S], COEF[j] / 2048, COEF[j] * (192 - 511.5 / 2048)
@@ -314,147 +340,173 @@ def rank_program(g, core, T, topo):
         act(T["gb%d" % J][:, S * j:S * j + S], Y[j][:, 0:S], AF.Copy, [YK[j]], ["gb%d%d" % (J, j)],
             bias=-COEF[j] * (192 + 512.5 / 2048), scale=-COEF[j] / 2048)
 
-    def wrap(J, j):
-        c = COEF[j] * (192 - MOD[j] * (192 - (MOD[j] - 1) / (2 * MOD[j])))
-        ts(T["f3%d" % J][:, S * j:S * j + S], T["ga%d" % J][:, S * j:S * j + S], -1.0, c, ALU.mult, ALU.add, ["ga%d%d" % (J, j)], ["f3%d%d" % (J, j)])
+    def wrap(J, j, on):
+        out = T["f3%d" % J][:, S * j:S * j + S]
+        if on == "a":
+            act(out, Y[j][:, 0:S], AF.Copy, [YK[j]], ["f3%d%d" % (J, j)],
+                bias=-COEF[j] * (512.5 / 2048 + 191.5 * MOD[j]), scale=-COEF[j] / 2048)
+        else:
+            c = COEF[j] * (192 - MOD[j] * (192 - (MOD[j] - 1) / (2 * MOD[j])))
+            ts(out, T["ga%d" % J][:, S * j:S * j + S], -1.0, c, ALU.mult, ALU.add, ["ga%d%d" % (J, j)], ["f3%d%d" % (J, j)])
 
-    def place_term(J, kind, j, st, sp):
-        mm(T.z[:, 0:S], T.id1[:], T["%s%d" % (kind, J)][:, S * j:S * j + S], st, sp, ["id1", "%s%d%d" % (kind, J, j)], ["@z"])
+    def place_terms(J, order, which=range(6)):
+        for i in which:
+            kind, j = order[i]
+            mm(T.z[:, 0:S], T.id1[:], T["%s%d" % (kind, J)][:, S * j:S * j + S], i == 0, i == 5, ["id1", "%s%d%d" % (kind, J, j)], ["@z"])
 
     def places(J):
         c = sum(192 * COEF[j] * (MOD[j] - 1) for j in range(3))
         ts(T["off%d" % J][:], T.z[:, 0:S], c, None, ALU.add, None, ["@z"], ["off%d" % J])
 
-    def score_start(J, t):
-        mm(SB[J][:, 0:S], T.id8k[:], T["live%d" % t][:], True, False, ["id8k", "live%d" % t], ["@s%d" % J])
-        for kind in ("ga", "gb"):
-            for j in range(3):
-                mm(SB[J][:, 0:S], CID[j][0][:], T["%s%d" % (kind, J)][:, S * j:S * j + S], False, False,
-                   [CID[j][1], "%s%d%d" % (kind, J, j)], ["@s%d" % J])
+    def score_terms(J, bank, x0, x1, terms, stop=False):
+        for i, (kind, j) in enumerate(terms):
+            mm(T[bank][:, x0:x1], CID[j][0][:], T["%s%d" % (kind, J)][:, S * j + x0:S * j + x1], False, stop and i == len(terms) - 1,
+               [CID[j][1], "%s%d%d" % (kind, J, j)], ["@" + bank])
 
-    def gather_a(J, b):
-        x0, x1 = CH[b]
-        act(T["gg%d" % J][:, 16 * x0:16 * x1], T.rfb[:].indirect(T["off%d" % J][:, x0:x1]), AF.Copy, ["off%d" % J], ["gg%d%d" % (J, b)], RF)
+    def score_start(J, t, bank, x0, x1, nb):
+        mm(T[bank][:, x0:x1], T.id8k[:], T["live%d" % t][:, x0:x1], True, False, ["id8k", "live%d" % t], ["@" + bank])
+        score_terms(J, bank, x0, x1, [("ga", j) for j in range(3)] + [("gb", j) for j in range(nb)])
 
-    def gather_v(J):
-        tt(T["pd%d" % J][:], T.rfb[:].indirect(T["off%d" % J][:, XA:S]), T.pfx[:], ALU.mult,
-           ["off%d" % J] + ["pfx%d" % m for m in range(16)], ["pd%d" % J], RF)
+    def pieces(J, names, r=None):
+        return ["pr%d%s%d" % (J, x, q) for x in names for q in (range(4) if r is None else [r])]
 
-    def sum_v(J):
-        for m in range(16):
-            mm(SB[J][:, XA:S], T.wd[:, 15 - m:143 - m], T["pd%d" % J][:, m::16], False, False, ["wd", "pd%d" % J], ["@s%d" % J])
+    def gather_a(J, name, x0, x1):
+        act(T["pr%d" % J][:, 16 * x0:16 * x1], T.rfb[:].indirect(T["off%d" % J][:, x0:x1]), AF.Copy, ["off%d" % J], pieces(J, name), RF)
 
-    def times(J, b, r):
-        x0, x1 = CH[b]
-        w = 4 * (x1 - x0)
-        o = 16 * x0 + r * w
-        tt(T["pa%d" % J][:, o:o + w], T["gg%d" % J][:, 16 * x0 + r:16 * x1:4], PF[b][:, 0:w], ALU.mult,
-           ["gg%d%d" % (J, b), "@pf%d" % b], ["pa%d%d%d" % (J, b, r)])
+    def gather_v(J, name, x0, x1):
+        tt(T["pr%d" % J][:, 16 * x0:16 * x1], T.rfb[:].indirect(T["off%d" % J][:, x0:x1]), T.pfx[:, 16 * (x0 - X0):16 * (x1 - X0)], ALU.mult,
+           ["off%d" % J] + ["pfx%d" % m for m in range(16)], pieces(J, name), RF)
 
-    def sum_a(J, b, r, last=False):
-        x0, x1 = CH[b]
-        w = 4 * (x1 - x0)
-        o = 16 * x0 + r * w
+    def times(J, names, r, x0, x1):
+        part = T["pr%d" % J][:, 16 * x0 + r:16 * x1:4]
+        tt(part, part, T.pf4[:, 4 * x0:4 * x1], ALU.mult, pieces(J, names, r) + ["@pf4"], pieces(J, names, r))
+
+    def sums(J, names, r, bank, x0, x1, stop=True):
         for i in range(4):
             m = r + 4 * i
-            mm(SB[J][:, x0:x1], T.wd[:, 15 - m:143 - m], T["pa%d" % J][:, o + i:o + w:4], False, last and i == 3,
-               ["wd", "pa%d%d%d" % (J, b, r)], ["@s%d" % J])
+            mm(T[bank][:, x0:x1], T.wd[:, 15 - m:143 - m], T["pr%d" % J][:, 16 * x0 + m:16 * x1:16], False, stop and r == 3 and i == 3,
+               ["wd"] + pieces(J, names, r), ["@" + bank])
 
-    def verdict(J, t):
-        name = ("so%d", "sf%d")[J] % t
-        act(T["nh%d" % J][:], SB[J][:, 0:S], AF.Sign, ["@s%d" % J, "thc"], ["nh%d" % J, name],
-            bias=T.thc[:, 0:1], scale=-1.0, accum_out=T[name][:, 0:1])
-        send(name)
+    def verdict(J, bank, x0, x1, out, key):
+        act(T["nh%d" % J][:, x0:x1], T[bank][:, x0:x1], AF.Sign, ["@" + bank, "thc"], ["nh" + key, key],
+            bias=T.thc[:, 0:1], scale=-1.0, accum_out=out)
 
-    def winner(J, here, far):
-        ext = [(far, arrive[far])]
-        a, b = T[here][:, 0:1], T[far][:, 0:1]
-        ts(T.k32[:], T.m32[:], a, b, ALU.add, ALU.add, ["m32", here], ["k32"], ext)
-        ts(T.kb[:], T.m128[:], a, b, ALU.add, ALU.add, ["m128", here], ["kb"])
+    def winner_early(J, one, ext=()):
+        rd = [] if ext else [one]
+        ts(T["tot%d" % J][:, 0:1], T[one][:, 0:1], T.col[:, 3:4], None, ALU.add, None, rd + ["col3"], ["tot%da" % J], ext)
+        ts(T["pk%d" % J][:], T.pen32[:], T["tot%d" % J][:, 0:1], None, ALU.add, None,
+           ["pen32%d" % q for q in range(0, 128, 32)] + ["tot%da" % J], ["pk%d" % J])
+
+    def winner(J, two, rd, ext=()):
+        a, b = T[two][:, 0:1], T[two][:, 1:2]
+        tot = T["tot%d" % J][:, 1:2]
+        ts(T.k32[:], T["pk%d" % J][:], a, b, ALU.add, ALU.add, ["pk%d" % J] + rd, ["k32"], ext)
+        ts(tot, T["tot%d" % J][:, 0:1], a, b, ALU.add, ALU.add, ["tot%da" % J] + rd, ["tot%db" % J])
         op("v", lambda: V.transpose(T.k32t[:], T.k32[:]), ["k32"], ["k32t"])
         op("v", lambda: V.tensor_reduce(T.mn[:, 0:1], T.k32t[:], AX.X, ALU.min), ["k32t"], ["mn"])
-        ts(T["win%d" % J][:], T.kb[:], T.mn[:, 0:1], None, ALU.is_le, None, ["kb", "mn"], ["win%d" % J])
+        ts(T["win%d" % J][:], T.pen[:], tot, T.mn[:, 0:1], ALU.add, ALU.is_le, ["pen", "mn", "tot%db" % J], ["win%d" % J])
 
-    pfx_pool(range(POOL_PRE))
+    pfx_copies("g0")
+    early_b = 3 - LATE_B
     for t in range(RO):
-        live = "live%d" % t
-        lattices(t)
-        send("tt%d" % t)
+        live, so, sf, ra, rb = ["%s%d" % (x, t) for x in ("live", "so", "sf", "ra", "rb")]
         if t == 0:
-            pfx_pool(range(POOL_PRE, POOL_PRE + POOL_POST))
-            for m in range(POOL_PRE + POOL_POST, 16):
-                act(T.pfx[:, m::16], T.pfb[:, XA:S], AF.Copy, [], ["pfx%d" % m], PFD)
-        for j in range(3):
-            spread(0, "tt%d" % t, j)
-            dots(0, j)
+            lattices(0, T.sell[0:8, :], 8, "lvb")
+            pfx_copies("g1")
+            pool_constants()
+            pfx_copies("a0")
+            ts(T.id1[:], T.uu[:], 0.0, None, ALU.is_equal, None, ["uu"], ["id1"])
+            ts(T.pc2[:, 0:1], T.pci[:, 0:1], 15, None, ALU.bitwise_and, None, ["pci"], ["m"])
+            ts(T.thc[:, 0:1], T.thi[:, 0:1], BIG - 0.5, None, ALU.add, None, [], ["thc"], TH)
+            ts(T.col[:, 3:4], T.pc2[:, 0:1], 1.0 / 32, None, ALU.mult, None, ["m"], ["col3"])
+            ts(T.col[:, 4:5], T.pc2[:, 0:1], -1.0 / 32, -2.0 * S, ALU.mult, ALU.add, ["m"], ["col4"])
+            pfx_copies("v0")
+        else:
+            lattices(t, T.win0[:], 128, "surv")
+        dots("ax%d" % t, ["ax%d" % t])
         floor_a(0, 0, "a")
         floor_a(0, 1, "a")
         floor_a(0, 2, "v")
-        wrap(0, 0)
-        wrap(0, 2)
-        wrap(0, 1)
-        for i, (kind, j) in enumerate([("ga", 0), ("ga", 2), ("ga", 1), ("f3", 0), ("f3", 2), ("f3", 1)]):
-            place_term(0, kind, j, i == 0, i == 5)
+        wrap(0, 0, "v")
+        wrap(0, 2, "v")
+        wrap(0, 1, "v")
+        place_terms(0, [("ga", 0), ("ga", 2), ("f3", 0), ("ga", 1), ("f3", 2), ("f3", 1)])
+        if t == 0:
+            pfx_copies("a1")
+            pfx_copies("v1")
         for j in range(3):
             floor_b(0, j)
         if t == 0:
-            late_constants()
+            for x0 in range(0, max(XA), 128):
+                x1 = min(x0 + 128, max(XA))
+                for i in range(4):
+                    mm(T.pf4[:, 4 * x0 + i:4 * x1:4], T.id1[:], T.pfb[:, x0:x1], True, True, ["id1"], ["@pf4"], PFD)
         places(0)
-        gather_a(0, 0)
-        gather_v(0)
-        score_start(0, t)
-        gather_a(0, 1)
-        sum_v(0)
-        for j in range(3):
-            spread(1, "rt%d" % t, j, [("rt%d" % t, arrive["rt%d" % t])])
-            dots(1, j)
-        for r in range(4):
-            times(0, 0, r)
-            sum_a(0, 0, r)
+        gather_a(0, "a", 0, XA[0])
+        gather_v(0, "v", XA[0], S)
+        dots("rt%d" % t, [], came("rt%d" % t))
+        score_start(0, t, "s0", 0, S, 3)
         for j in range(3):
             floor_a(1, j, "a")
-        for r in range(2):
-            times(0, 1, r)
-            sum_a(0, 1, r)
-        for j in range(3):
-            place_term(1, "ga", j, j == 0, False)
-        for j in range(3):
-            wrap(1, j)
-            place_term(1, "f3", j, False, j == 2)
-        for j in range(3):
-            floor_b(1, j)
-        times(0, 1, 2)
+            wrap(1, j, "a")
+        order = [(k, j) for j in range(3) for k in ("ga", "f3")]
+        for r in range(4):
+            times(0, "a", r, 0, XA[0])
+            sums(0, "v", r, "s0", XA[0], S, False)
+            if r < 3:
+                place_terms(1, order, (2 * r, 2 * r + 1))
         places(1)
-        sum_a(0, 1, 2)
-        times(0, 1, 3)
-        sum_a(0, 1, 3, True)
-        gather_a(1, 0)
-        gather_v(1)
-        score_start(1, t)
-        verdict(0, t)
-        gather_a(1, 1)
-        sum_v(1)
-        mm(T.y0[:, 0:S], T.id8k[:], T[live][:], True, False, ["id8k", live], ["@y0"])
-        mm(T.y0[:, 0:S], T.id1[:], T.nh0[:], False, False, ["id1", "nh0"], ["@y0"])
-        if t == RO - 1:
-            for u in range(RO):
-                mm(T.z[0:8, 0:S], T.id1[:, ::16], T["live%d" % u][:], u == 0, False, ["id1", "live%d" % u], ["@z"])
-        for b in range(2):
-            for r in range(4):
-                times(1, b, r)
-                sum_a(1, b, r, b == 1 and r == 3)
-        ts(T.own2[:, 0:1], T["so%d" % t][:, 0:1], -2.0 * S, None, ALU.add, None, ["so%d" % t], ["own2"])
-        verdict(1, t)
-        winner(1, "sf%d" % t, "ra%d" % t)
-        mm(T.y0[:, 0:S], T.win1[:], T.nh1[:], False, True, ["win1", "nh1"], ["@y0"])
-        ts(T.surv[:], T.y0[:, 0:S], BIG + 1.5, None, ALU.is_ge, None, ["@y0"], ["surv"])
-        winner(0, "so%d" % t, "rb%d" % t)
+        for r in range(4):
+            sums(0, "a", r, "s0", 0, XA[0])
+        for j in range(early_b):
+            floor_b(1, j)
+        gather_v(1, "v", XA[1], S)
+        gather_a(1, "a", L1, XA[1])
+        verdict(0, "s0", 0, S, T[so][:, 0:1], so)
+        send(so, [so])
+        gather_a(1, "b", L, L1)
+        gather_a(1, "c", 0, L)
+        score_start(1, t, "s1", L, S, early_b)
+        score_start(1, t, "z", 0, L, early_b)
+        mm(T.s0[:, 0:S], T.id8k[:], T[live][:], True, False, ["id8k", live], ["@s0"])
+        mm(T.s0[:, 0:S], T.id1[:], T.nh0[:], False, False, ["id1", "nh" + so], ["@s0"])
+        for r in range(4):
+            sums(1, "v", r, "s1", XA[1], S, False)
+        for r in range(4):
+            times(1, "a", r, L1, XA[1])
+            sums(1, "a", r, "s1", L1, XA[1], False)
+        for r in range(4):
+            times(1, "b", r, L, L1)
+            sums(1, "b", r, "s1", L, L1, LATE_B == 0)
+        winner_early(0, so)
+        late = [("gb", j) for j in range(early_b, 3)]
+        for j in range(early_b, 3):
+            floor_b(1, j)
+        for r in range(4):
+            times(1, "c", r, 0, L)
+            if r == 2:
+                score_terms(1, "s1", L, S, late, True)
+                score_terms(1, "z", 0, L, late)
+            sums(1, "c", r, "z", 0, L)
+        verdict(1, "s1", L, S, T[sf][:, 0:1], sf + "a")
+        verdict(1, "z", 0, L, T[sf][:, 1:2], sf + "b")
+        send(sf, [sf + "a", sf + "b"])
         if t < RO - 1:
-            mm(T.z[:, 0:S], T.win0[:], T.surv[:], True, True, ["win0", "surv"], ["@z"])
+            thresholds(t + 1)
         else:
-            mm(T.z[0:8, 0:S], T.win0[:, ::16], T.surv[:], False, True, ["win0", "surv"], ["@z"])
-        ts(T.ycs[:, t:t + 1], T.own2[:, 0:1], T["rb%d" % t][:, 0:1], -0.5, ALU.add, ALU.mult, ["own2"], ["ycs%d" % t])
-    cp(T.yas[0:8, :], T.z[0:8, 0:S], ["@z"], ["yas"])
+            for u in range(RO):
+                mm(T.y0[0:8, 0:S], T.id1[:, ::16], T["live%d" % u][:], u == 0, False, ["id1", "live%d" % u], ["@y0"])
+        winner_early(1, ra, came(ra))
+        winner(1, sf, [sf + "a", sf + "b"])
+        mm(T.s0[:, 0:S], T.win1[:], T.nh1[:], False, True, ["win1", "nh" + sf + "a", "nh" + sf + "b"], ["@s0"])
+        ts(T.surv[:], T.s0[:, 0:S], BIG + 1.5, None, ALU.is_ge, None, ["@s0"], ["surv"])
+        if t < RO - 1:
+            scan(T.cum[:], T.surv[:], T.surv[:], ALU.add, ALU.max, ["surv"], ["cum"])
+        winner(0, rb, [], came(rb))
+        if t == RO - 1:
+            mm(T.y0[0:8, 0:S], T.win0[:, ::16], T.surv[:], False, True, ["win0", "surv"], ["@y0"])
+        ts(T.ycs[:, t:t + 1], T.tot0[:, 1:2], T.col[:, 4:5], -0.5, ALU.add, ALU.mult, ["tot0b", "col4"], ["ycs%d" % t])
+    cp(T.yas[0:8, :], T.y0[0:8, 0:S], ["@y0"], ["yas"])
     op("a", lambda: g.scalar.dma_start(T.yc[:], T.ycs[:, 0:RO]).then_inc(T.sem.d_out, 16), ["ycs%d" % t for t in range(RO)], [])
     op("s", lambda: g.sync.dma_start(T.ya[:], T.yas[0:8, :]).then_inc(T.sem.d_out, 16), ["yas"], [])
     emit(ops, {"v": V, "a": A, "p": P, "g": g, "s": g.sync}, T)

@@ -2,16 +2,21 @@ from concourse.mybir import AluOpType as ALU, AxisListType as AX, ActivationFunc
 
 S = 384
 RO = 2
-XA = [192, 240]
-X0 = min(XA)
+XA = [[160, 192], [150, 192]]
+XH, X0 = XA[0][0], min(XA[0] + XA[1])
 XD = S - X0
-L1, L = 152, 64
+U = 360
+F0 = [250, 180]
+F1 = 330
+GA = 56
+L = [84, 64]
 LATE_B = 1
+AXES = ["gs0", "ax0"]
 COEF = [128.0, 8.0, 1.0]
 MOD = [16.0, 16.0, 8.0]
 BIG = 8192.0
-WB = 400
-COPIES = {"g0": 4, "g1": 2, "a0": 3, "a1": 2, "v0": 2, "v1": 3}
+WB = S + 1
+COPIES = {"g0": 3, "g1": 2, "a0": 4, "a1": 1, "v0": 3, "v1": 3}
 
 SCRATCH = {
     "posb": ("sbuf", [128, S], "bfloat16"), "tb": ("sbuf", [128, S], "bfloat16"),
@@ -22,37 +27,38 @@ SCRATCH = {
     "pfx": ("sbuf", [128, 16 * XD], "bfloat16"),
     "qp": ("sbuf", [128, 96], "bfloat16"), "qm": ("sbuf", [128, 96], "bfloat16"), "sel": ("sbuf", [128, 384], "bfloat16"),
     "sgn": ("sbuf", [128, 128], "bfloat16"), "sb1": ("sbuf", [128, 128], "bfloat16"), "sb2": ("sbuf", [128, 128], "bfloat16"),
-    "pci": ("sbuf", [128, 8], "int32"), "pc2": ("sbuf", [128, 8], "int32"), "sb3": ("sbuf", [128, 128], "bfloat16"),
+    "pci": ("sbuf", [128, 8], "int32"), "pc2": ("sbuf", [128, 8], "int32"),
+    "sel4": ("sbuf", [128, 128], "bfloat16"), "pen4": ("sbuf", [128, 128], "bfloat16"), "win4": ("sbuf", [128, 128], "bfloat16"),
     "col": ("sbuf", [128, 8], "float32"), "k2": ("sbuf", [128, 8], "float32"), "blk": ("sbuf", [128, 16], "bfloat16"),
     "uu": ("sbuf", [128, 128], "bfloat16"), "u2": ("sbuf", [128, 128], "bfloat16"), "zero": ("sbuf", [128, 128], "bfloat16"),
     "pen1": ("sbuf", [128, 128], "bfloat16"),
     "offe": ("sbuf", [128, 8], "uint16"), "thr": ("sbuf", [128, 128], "bfloat16"),
     "cst": ("sbuf", [128, S], "bfloat16"), "ramp": ("sbuf", [128, S], "float16"),
     "sell": ("sbuf", [128, 128], "float16"), "wd": ("sbuf", [128, 144], "bfloat16"),
-    "id1": ("sbuf", [128, 128], "bfloat16"), "id64": ("sbuf", [128, 128], "bfloat16"),
-    "id1k": ("sbuf", [128, 128], "bfloat16"), "id8k": ("sbuf", [128, 128], "bfloat16"),
-    "pen32": ("sbuf", [128, 32], "bfloat16"), "pen": ("sbuf", [128, 128], "bfloat16"),
+    "id1": ("sbuf", [128, 128], "bfloat16"), "id8k": ("sbuf", [128, 128], "bfloat16"),
+    "id128": ("sbuf", [128, 128], "bfloat16"), "id8": ("sbuf", [128, 128], "bfloat16"),
+    "thb": ("sbuf", [128, 8], "bfloat16"), "thd": ("sbuf", [128, 256], "bfloat16"), "nt": ("sbuf", [128, S], "bfloat16"),
+    "nh0": ("sbuf", [128, S], "bfloat16"), "nh1": ("sbuf", [128, S], "bfloat16"),
+    "one": ("sbuf", [128, 8], "bfloat16"), "tot": ("sbuf", [128, 8], "float32"), "pen32": ("sbuf", [128, 33], "bfloat16"), "pen": ("sbuf", [128, 128], "bfloat16"),
     "cum": ("sbuf", [128, S], "float16"), "junk": ("sbuf", [128, S], "bfloat16"), "sc": ("sbuf", [128, 2 * S], "float16"),
-    "cnt": ("sbuf", [128, 8], "float32"), "offs": ("sbuf", [128, 8], "uint16"), "gs": ("sbuf", [128, 96], "bfloat16"),
+    "cnt": ("sbuf", [128, 8], "float32"), "offs": ("sbuf", [128, 8], "uint16"),
     "live0": ("sbuf", [128, S], "bfloat16"), "live1": ("sbuf", [128, S], "bfloat16"), "surv": ("sbuf", [128, S], "float16"),
-    "k32": ("sbuf", [128, 32], "float32"), "k32t": ("sbuf", [128, 32], "float32"),
+    "key0": ("sbuf", [128, 33], "float32"), "key1": ("sbuf", [128, 33], "float32"), "k32t": ("sbuf", [128, 32], "float32"),
     "mn": ("sbuf", [128, 8], "float32"), "win0": ("sbuf", [128, 128], "float16"), "win1": ("sbuf", [128, 128], "bfloat16"),
-    "ycs": ("sbuf", [128, 8], "float32"), "yas": ("sbuf", [128, S], "float32"),
-    "y0": ("psum", [128, 512], "float32"), "y1": ("psum", [128, 512], "float32"), "y2": ("psum", [128, 512], "float32"),
+    "ycs": ("sbuf", [128, 8], "float32"), "yas": ("sbuf", [128, S // 4], "float32"),
+    "y": ("psum", [128, 3, 512], "float32"),
     "z": ("psum", [128, 512], "float32"), "s0": ("psum", [128, 512], "float32"), "s1": ("psum", [128, 512], "float32"),
-    "pf4": ("psum", [128, 1024], "float32"),
+    "pf8": ("psum", [128, 1024, 2], "bfloat16"), "pf2": ("sbuf", [128, 512], "bfloat16"), "pft": ("sbuf", [128, 512], "bfloat16"),
 }
 for _j in range(2):
-    SCRATCH["ga%d" % _j] = ("sbuf", [128, 3 * S], "bfloat16")
-    SCRATCH["gb%d" % _j] = ("sbuf", [128, 3 * S], "bfloat16")
-    SCRATCH["f3%d" % _j] = ("sbuf", [128, 3 * S], "bfloat16")
+    SCRATCH["ga%d" % _j] = ("sbuf", [128, 3, S], "bfloat16")
+    SCRATCH["gb%d" % _j] = ("sbuf", [128, 3, S], "bfloat16")
+    SCRATCH["f3%d" % _j] = ("sbuf", [128, 3, S], "bfloat16")
+    SCRATCH["ax%d" % _j] = ("sbuf", [128, 384], "bfloat16")
     SCRATCH["off%d" % _j] = ("sbuf", [128, S], "uint16")
     SCRATCH["pr%d" % _j] = ("sbuf", [128, 16 * S], "bfloat16")
-    SCRATCH["nh%d" % _j] = ("sbuf", [128, S], "bfloat16")
-    SCRATCH["pk%d" % _j] = ("sbuf", [128, 32], "float32")
-    SCRATCH["tot%d" % _j] = ("sbuf", [128, 8], "float32")
 for _t in range(RO):
-    SCRATCH["ax%d" % _t] = ("sbuf", [128, 384], "bfloat16")
+    SCRATCH["gs%d" % _t] = ("sbuf", [128, 96], "bfloat16")
     SCRATCH["rt%d" % _t] = ("sbuf", [128, 384], "bfloat16")
     SCRATCH["so%d" % _t] = ("sbuf", [128, 8], "float32")
     SCRATCH["sf%d" % _t] = ("sbuf", [128, 8], "float32")
@@ -80,15 +86,22 @@ def routes(rank, T, topo):
     msgs = []
     for t in range(RO):
         nxt, prv = T.cores[(rank + t + 1) % n], T.cores[(rank - t - 1) % n]
-        msgs += [("ax%d" % t, "rt%d" % t, 384, nxt), ("so%d" % t, "ra%d" % t, 1, nxt), ("sf%d" % t, "rb%d" % t, 2, prv)]
+        msgs += [(AXES[t], "rt%d" % t, 96 if AXES[t][0] == "g" else 384, nxt), ("so%d" % t, "ra%d" % t, 1, nxt), ("sf%d" % t, "rb%d" % t, 1, prv)]
     barred = [m[3] for m in msgs if not topo.may_write(src, m[3])]
     via = relay_of(src, barred, T, topo) if barred else None
     return [m + ((None if topo.may_write(src, m[3]) else via),) for m in msgs]
 
 
+def mask_of(topo, src, dst, name):
+    e = topo.engines(src, dst)
+    if name == "rt0" and dst in topo.cores_of(src):
+        e = e[:len(e) // 2]
+    return sum(1 << x for x in e)
+
+
 def remote(g, T, topo, src, dst, out_name, in_name, cols):
     rid, pid = topo.addr(dst, src)
-    m = topo.mask(src, dst)
+    m = mask_of(topo, src, dst, out_name)
     g.remote_dma(T[out_name][:, 0:cols], T[in_name][:, 0:cols], T.sem[out_name], T.sem.sent, pid, rid, m)
     return bits(m)
 
@@ -98,7 +111,7 @@ def relay_program(g, core, T, topo):
     for r in range(len(T.cores)):
         for (_, far, cols, dst, via) in routes(r, T, topo):
             if via == core:
-                g.wait_ge(T.sem[far], bits(topo.mask(T.cores[r], core)))
+                g.wait_ge(T.sem[far], bits(mask_of(topo, T.cores[r], core, far)))
                 total += remote(g, T, topo, core, dst, far, far, cols)
     if total:
         g.wait_ge(T.sem.sent, total)
@@ -216,70 +229,77 @@ def rank_program(g, core, T, topo):
     def came(name):
         return [(name, arrive[name])]
 
-    Y = [T.y0, T.y1, T.y2]
-    YK = ["@y0", "@y1", "@y2"]
-    CID = [(T.id64, "id64"), (T.id1k, "id1k"), (T.id8k, "id8k")]
+    def bk(name):
+        return T.y[:, int(name[1]), 0:S] if name[0] == "y" else T[name][:, 0:S]
+
+    CID = ["id128", "id8", "id1"]
 
     g.sync.dma_start(T.lvi[0:8, :], T.lv[:]).then_inc(T.sem.d_lv, 16)
     g.scalar.dma_start(T.posb[0:24, :], T.pos[:]).then_inc(T.sem.d_pos, 16)
     g.sync.dma_start(T.pfb[:], T.pf[:]).then_inc(T.sem.d_pf, 16)
-    g.sync.dma_start(T.rfb[:], T.rf[:]).then_inc(T.sem.d_rf, 16)
-    g.scalar.dma_start(T.thi[:, 0:1], T.th[:]).then_inc(T.sem.d_th, 16)
+    g.scalar.dma_start(T.rfb[:, 0:2048], T.rf[:]).then_inc(T.sem.d_rf, 16)
+    g.sync.dma_start(T.thi[:, 0:1], T.th[:]).then_inc(T.sem.d_th, 16)
     LV, POS, PFD, TH, RF = [("d_lv", 16)], [("d_pos", 16)], [("d_pf", 16)], [("d_th", 16)], [("d_rf", 16)]
 
-    COUNT = [("s0", "z", "s1", "y0"), ("y0", "y2", "y1", "s1")]
+    COUNT = [("s0", "z", "s1", "s0"), ("y0", "y2", "y1", "s1")]
 
-    def thresholds(t):
-        for bank, r in zip(COUNT[t], (0, 2, 1)):
-            mm(T[bank][:, 0:S], T.thr[32 * r:32 * r + 1, :], T.cst[32 * r:32 * r + 1, :], True, False, ["thr", "cst"], ["@" + bank, "!" + bank])
+    def thresholds(t, which):
+        for i in which:
+            bank, r = COUNT[t][i], (0, 2, 1)[i]
+            mm(bk(bank), T.thr[32 * r:32 * r + 1, :], T.cst[32 * r:32 * r + 1, :], True, False, ["thr", "cst"], ["@" + bank, "!" + bank])
 
-    iota(T.thr[0:96, :], [[0, 8], [3072, 16]], 512, 32, ["thr"])
     iota(T.qp[0:24, 0:48], [[-1, 3], [-3, 8], [0, 2]], 0, 1, ["qp0"])
     iota(T.qm[0:24, 0:48], [[1, 3], [-3, 8], [0, 2]], -2, 1, ["qm0"])
-    iota(T.sgn[0:24, :], [[0, 8], [-2, 2], [0, 8]], 1, 0, ["sgn"])
+    iota(T.sgn[0:32, :], [[0, 8], [-2, 2], [0, 8]], 1, 0, ["sgn"])
+    iota(T.thr[0:96, :], [[0, 8], [3072, 16]], 512, 32, ["thr"])
     iota(T.u2[0:8, :], [[-1, 8], [0, 16]], 0, 1, ["u2"])
     iota(T.pci[:, 0:4], [[128, 4]], 0, 1, ["pci"], False)
+    iota(T.k2[:, 0:2], [[2 * WB, 2]], S, 0, ["k2"])
     iota(T.uu[:], [[-1, 128]], 0, 1, ["uu"])
     ms(T.cst[:], -1.0 / 1024, ["cst"])
-    for c in (6, 7):
-        ms(T.sel[0:24, c::8], 0.0, ["sel%d" % c])
-    scan(T.ramp[:], T.cst[:], T.cst[:], ALU.add, ALU.min, ["cst"], ["ramp"])
-    thresholds(0)
+    ms(T.sel[0:32, 128:256], -192.0, ["sel"])
     cp(T.qp[0:24, 48:96], T.qp[0:24, 0:48], ["qp0"], ["qp1"])
-    for c in range(3):
-        ts(T.sel[0:24, c::8], T.qp[0:24, 16 * c:16 * c + 48], 0.0, None, ALU.is_equal, None, ["qp0", "qp1"], ["sel%d" % c])
+    for c in (6, 7):
+        act(T.sel[0:24, c::8], T.cst[0:24, 0:48], AF.Copy, ["cst", "sel"], ["sel%d" % c], scale=0.0)
     cp(T.qm[0:24, 48:96], T.qm[0:24, 0:48], ["qm0"], ["qm1"])
     for c in range(3):
-        ts(T.sel[0:24, 3 + c:256:8], T.qm[0:24, 32 - 16 * c:64 - 16 * c], 0.0, None, ALU.is_equal, None, ["qm0", "qm1"], ["sel%d" % (3 + c)])
+        ts(T.sel[0:24, c::8], T.qp[0:24, 16 * c:16 * c + 48], 0.0, None, ALU.is_equal, None, ["qp0", "qp1", "sel"], ["sel%d" % c])
+    for c in range(3):
+        ts(T.sel[0:24, 3 + c:256:8], T.qm[0:24, 32 - 16 * c:64 - 16 * c], 0.0, None, ALU.is_equal, None, ["qm0", "qm1", "sel"], ["sel%d" % (3 + c)])
+    SELK = ["sel%d" % r for r in range(8)]
+    tt(T.sb2[0:32, :], T.sel[0:32, 128:256], T.sgn[0:32, :], ALU.mult, SELK + ["sgn"], ["sb2"])
+    act(T.tb[0:32, :], T.cst[0:32, :], AF.Copy, ["cst"], ["tb"], scale=0.0, bias=1.0)
+    act(T.w[:, S::WB], T.cst[:, 0:2], AF.Copy, ["cst"], ["wz"], scale=0.0)
+    act(T.ax0[:], T.cst[:], AF.Copy, ["cst"], ["ax0"], scale=0.0)
+    act(T.tb[0:24, :], T.posb[0:24, :], AF.Copy, [], ["tb"], POS, bias=1536.0)
+    cp(T.lvb[0:8, :], T.lvi[0:8, :], [], ["lvb"], LV)
+    ts(T.sb1[0:24, :], T.sb2[0:24, :], -1.0, 0.0, ALU.mult, ALU.max, ["sb2"], ["sb1"])
+    scan(T.cum[0:8, :], T.lvb[0:8, :], T.lvb[0:8, :], ALU.add, ALU.max, ["lvb"], ["cum"])
+    ts(T.sell[0:8, :], T.u2[0:8, :], 0.0, None, ALU.is_equal, None, ["u2"], ["sell"])
+    scan(T.ramp[:], T.cst[:], T.cst[:], ALU.add, ALU.min, ["cst"], ["ramp"])
     for c in range(3):
         ts(T.sel[0:24, 259 + c::8], T.qm[0:24, 64 - 16 * c:80 - 16 * c], 0.0, -1.0, ALU.is_equal, ALU.mult, ["qm0", "qm1"], ["selr%d" % c])
-    SELK = ["sel%d" % r for r in range(8)]
-    tt(T.sb2[0:24, :], T.sel[0:24, 128:256], T.sgn[0:24, :], ALU.mult, SELK + ["sgn"], ["sb2"])
-    ts(T.sb1[0:24, :], T.sb2[0:24, :], -1.0, 0.0, ALU.mult, ALU.max, ["sb2"], ["sb1"])
-    cp(T.lvb[0:8, :], T.lvi[0:8, :], [], ["lvb"], LV)
-    ts(T.sell[0:8, :], T.u2[0:8, :], 0.0, None, ALU.is_equal, None, ["u2"], ["sell"])
-    scan(T.cum[0:8, :], T.lvb[0:8, :], T.lvb[0:8, :], ALU.add, ALU.max, ["lvb"], ["cum"])
-    act(T.ax0[:], T.cst[:], AF.Copy, ["cst"], ["ax0"], scale=0.0)
-    for i in range(2):
-        act(T.k2[:, i:i + 1], T.cst[:, 0:1], AF.Copy, ["cst"], ["k2%d" % i], scale=0.0, bias=float(S + 2 * WB * i))
-        act(T.w[:, WB * i + S:WB * i + WB], T.cst[:, 0:WB - S], AF.Copy, ["cst"], ["wz%d" % i], scale=0.0)
-    act(T.sb3[0:1, :], T.sgn[0:1, :], AF.Copy, ["sgn"], ["sb3"], scale=1536.0 * 1024)
-    act(T.tb[0:24, :], T.posb[0:24, :], AF.Copy, [], ["tb"], POS, bias=1536.0)
-    mm(T.y0[:, 0:S], T.sel[0:24, 0:128], T.posb[0:24, :], True, True, SELK, ["@y0"], POS)
-    mm(T.y1[:, 0:S], T.sb3[0:1, :], T.cst[0:1, :], True, False, ["sb3", "cst"], ["@y1"])
-    mm(T.y1[:, 0:S], T.sb1[0:24, :], T.posb[0:24, :], False, False, ["sb1"], ["@y1"])
-    mm(T.y1[:, 0:S], T.sb2[0:24, :], T.tb[0:24, :], False, True, ["sb2", "tb"], ["@y1"])
-    act(T.w[:, 0:S], T.y0[:, 0:S], AF.Copy, ["@y0"], ["wa"])
-    act(T.w[:, WB:WB + S], T.y1[:, 0:S], AF.Copy, ["@y1"], ["wb"])
+
+    def columns():
+        ts(T.col[:, 3:4], T.pc2[:, 0:1], 1.0 / 32, None, ALU.mult, None, ["m"], ["col3"])
+        ts(T.col[:, 4:5], T.pc2[:, 0:1], -1.0 / 32, -2.0 * S, ALU.mult, ALU.add, ["m"], ["col4"])
+
+    thresholds(0, [0])
+    mm(bk("y0"), T.sel[0:24, 0:128], T.posb[0:24, :], True, True, SELK, ["@y0"], POS)
+    thresholds(0, [1, 2])
+    mm(bk("y1"), T.sb2[0:32, :], T.tb[0:32, :], True, False, ["sb2", "tb"], ["@y1"])
+    mm(bk("y1"), T.sb1[0:24, :], T.posb[0:24, :], False, True, ["sb1"], ["@y1"])
+    act(T.w[:, 0:S], bk("y0"), AF.Copy, ["@y0"], ["wa"])
+    act(T.w[:, WB:WB + S], bk("y1"), AF.Copy, ["@y1"], ["wb"])
 
     todo = list(range(16))
 
     def pfx_copies(who):
         for _ in range(COPIES[who]):
             m = todo.pop()
-            out, src = T.pfx[:, m::16], T.pfb[:, X0:S]
+            out, src = T.pfx[:, 16 * (XH - X0) + m::16], T.pfb[:, XH:S]
             if who[0] == "g":
-                op("g", lambda out=out: g.affine_select(out, src, [[0, XD]], ALU.is_gt, 0.0, 1, 0), [], ["pfx%d" % m], PFD)
+                op("g", lambda out=out: g.affine_select(out, src, [[0, S - XH]], ALU.is_gt, 0.0, 1, 0), [], ["pfx%d" % m], PFD)
             elif who[0] == "a":
                 act(out, src, AF.Copy, [], ["pfx%d" % m], PFD)
             else:
@@ -288,123 +308,253 @@ def rank_program(g, core, T, topo):
     def select(out, src, pat, cmp, fill, base, cm, rd, wr):
         op("g", lambda: g.affine_select(out, src, pat, cmp, fill, base, cm), rd, wr)
 
+    NC = (max(XA[0] + XA[1]) + 63) // 64
+
     def pool_constants():
-        iota(T.zero[:], [[0, 128]], 0, 0, ["zero"])
-        for j in range(3):
-            select(CID[j][0][:], T.zero[:], [[-1, 128]], ALU.not_equal, BIG / COEF[j], 0, 1, ["zero"], [CID[j][1]])
-        iota(T.ax1[:], [[0, 384]], 0, 0, ["ax1"])
+        iota(T.blk[:, 8:16], [[0, 8]], 1, 0, ["blk1"])
+        for i in range(2):
+            select(T.pf2[:, i:128 * NC:2], T.pfb[:, 0:64 * NC], [[0, 64 * NC]], ALU.is_gt, 0.0, 1, 0, [], ["pf2%d" % i])
+        select(T.blk[:, 0:8], T.blk[:, 8:16], [[-16, 8]], ALU.is_ge, 0.0, 0, 1, ["blk1"], ["blk0"])
         iota(T.wd[:], [[0, 144]], 0, 0, ["wd0"])
-        iota(T.blk[:, 0:8], [[0, 8]], 1, 0, ["blk0"])
-        select(T.blk[:, 8:16], T.blk[:, 0:8], [[-16, 8]], ALU.is_ge, 0.0, 0, 1, ["blk0"], ["blk1"])
-        select(T.wd[:, 15:143:16], T.blk[:, 8:16], [[16, 8]], ALU.is_ge, 0.0, 15, -1, ["blk1", "wd0"], ["wd"])
+        select(T.blk[:, 8:16], T.blk[:, 0:8], [[16, 8]], ALU.is_ge, 0.0, 15, -1, ["blk0"], ["blk1"])
+        iota(T.ax1[:], [[0, 384]], 0, 0, ["ax1"])
+        select(T.wd[:, 15:143:16], T.blk[:, 8:16], [[0, 8]], ALU.is_gt, 0.0, 1, 0, ["blk1", "wd0"], ["wd"])
+        iota(T.zero[:], [[0, 128]], 0, 0, ["zero"])
+        for m in range(16 if XH > X0 else 0):
+            select(T.pfx[:, m:16 * (XH - X0):16], T.pfb[:, X0:XH], [[0, XH - X0]], ALU.is_gt, 0.0, 1, 0, [], ["pfy%d" % m])
         select(T.pen1[:], T.zero[:], [[-16, 8], [0, 16]], ALU.is_ge, 4096.0, 0, 1, ["zero"], ["pen1"])
         select(T.pen[:], T.pen1[:], [[16, 8], [0, 16]], ALU.is_ge, 4096.0, 15, -1, ["pen1"], ["pen"])
+        four, back = [[200, 4], [-16, 8], [-200, 4]], [[-200, 4], [16, 8], [200, 4]]
+        select(T.sel4[:], T.zero[:], four, ALU.not_equal, 1.0, 0, 1, ["zero"], ["sel4"])
+        select(T.pen1[:], T.zero[:], four, ALU.is_ge, 4096.0, 0, 1, ["zero"], ["pen1"])
+        select(T.pen4[:], T.pen1[:], back, ALU.is_ge, 4096.0, 15, -1, ["pen1"], ["pen4"])
+        iota(T.one[:, 0:1], [[0, 1]], 1, 0, ["one"])
+        iota(T.pen32[:, 0:1], [[0, 1]], 0, 0, ["pen32128"])
         for q in range(0, 128, 32):
-            select(T.pen32[q:q + 32, :], T.pen[q:q + 32, q:q + 32], [[0, 32]], ALU.is_gt, 0.0, 1, 0, ["pen"], ["pen32%d" % q])
+            select(T.pen32[q:q + 32, 1:33], T.pen[q:q + 32, q:q + 32], [[0, 32]], ALU.is_gt, 0.0, 1, 0, ["pen", "pen32128"], ["pen32%d" % q])
 
-    def lattices(t, pick, k, flags):
-        live, key = "live%d" % t, ("sell", "win0")[t]
+    def spread(ax, gs, rd, ext=()):
+        tt(T[ax][:].indirect(T.offe[:, 0:3]), T[gs][:, 0:48], T[gs][:, 48:96], ALU.mult, rd + ["offe"], [ax], ext)
+
+    def flags(t):
+        act(T["live%d" % t][:], bk(COUNT[t][3]), AF.Copy, ["@" + COUNT[t][3]], ["live%d" % t])
+
+    def lattices(t, pick, k, src):
+        key, gs = ("sell", "win0")[t], "gs%d" % t
         b0, b2, b1, bl = COUNT[t]
         for bank in (b0, b2, b1):
-            mm(T[bank][:, 0:S], pick, T.cum[0:k, :], False, True, [key, "cum", "!" + bank], ["@" + bank])
+            mm(bk(bank), pick, T.cum[0:k, :], False, True, [key, "cum", "!" + bank], ["@" + bank])
         if t == 0:
-            mm(T.y2[:, 0:S], T.sel[0:24, 256:384], T.posb[0:24, :], True, True, SELK + ["selr%d" % c for c in range(3)], ["@y2"])
-        mm(T[bl][:, 0:S], pick, T[flags][0:k, :], True, True, [key, flags], ["@" + bl])
-        scan(T.sc[:, 0:S], T[b0][:, 0:S], T.ramp[:], ALU.min, ALU.max, ["@" + b0, "ramp"], ["sc0"])
-        act(T.junk[:], T[b2][:, 0:S], AF.Sign, ["@" + b2], ["cnt", "junk"], scale=-1.0, accum_out=T.cnt[:, 0:1])
-        scan(T.sc[:, S:2 * S], T[b1][:, 0:S], T.ramp[:], ALU.min, ALU.max, ["@" + b1, "ramp"], ["sc1"])
-        ts(T.offs[:, 0:6:5], T.k2[:, 0:2], T.cnt[:, 0:1], 0.5, ALU.add, ALU.mult, ["k20", "k21", "cnt"], ["offs0"])
+            mm(bk("y2"), T.sel[0:24, 256:384], T.posb[0:24, :], True, True, SELK + ["selr%d" % c for c in range(3)], ["@y2"])
+        scan(T.sc[:, 0:S], bk(b0), T.ramp[:], ALU.min, ALU.max, ["@" + b0, "ramp"], ["sc0"])
+        mm(bk(bl), pick, T[src][0:k, :], True, True, [key, src], ["@" + bl])
+        act(T.junk[:], bk(b2), AF.Sign, ["@" + b2], ["cnt", "junk"], scale=-1.0, accum_out=T.cnt[:, 0:1])
+        scan(T.sc[:, S:2 * S], bk(b1), T.ramp[:], ALU.min, ALU.max, ["@" + b1, "ramp"], ["sc1"])
+        ts(T.offs[:, 0:6:5], T.k2[:, 0:2], T.cnt[:, 0:1], 0.5, ALU.add, ALU.mult, ["k2", "cnt"], ["offs0"])
         ts(T.offs[:, 1:3], T.sc[:, S - 1::S], -1024.0, None, ALU.mult, None, ["sc0", "sc1"], ["offs1"])
         ts(T.offs[:, 3:5], T.sc[:, S - 1::S], -1024.0, float(WB), ALU.mult, ALU.add, ["sc0", "sc1"], ["offs3"])
         if t == 0:
             cp(T.offe[:, 0:4], T.pci[:, 0:4], ["pci"], ["offe"])
-            act(T.posr[:], T.y2[:, 0:S], AF.Copy, ["@y2"], ["posr"])
-        act(T[live][:], T[bl][:, 0:S], AF.Copy, ["@" + bl], [live])
-        cp(T.gs[:], T.w[:].indirect(T.offs[:, 0:6]), ["wa", "wb", "wz0", "wz1", "offs0", "offs1", "offs3"], ["gs"])
-        tt(T["ax%d" % t][:].indirect(T.offe[:, 0:3]), T.gs[:, 0:48], T.gs[:, 48:96], ALU.mult, ["gs", "offe"], ["ax%d" % t])
-        send("ax%d" % t, ["ax%d" % t])
+            act(T.posr[:], bk("y2"), AF.Copy, ["@y2"], ["posr"])
+        else:
+            flags(t)
+        cp(T[gs][:], T.w[:].indirect(T.offs[:, 0:6]), ["wa", "wb", "wz", "offs0", "offs1", "offs3"], [gs])
+        if t == 0:
+            ts(T.pc2[:, 0:1], T.pci[:, 0:1], 15, None, ALU.bitwise_and, None, ["pci"], ["m"])
+        spread("ax0", gs, [gs])
+        send(AXES[t], [AXES[t]])
 
-    def dots(src, rd, ext=()):
-        for j in range(3):
+    now = [0]
+
+    def parts(J):
+        x = XA[now[0]][J]
+        return [(0, S)] if J else [(x, S), (0, x)]
+
+    def span(J, blocks):
+        xs, js = [x for p, j in blocks for x in parts(J)[p]], sorted(set(j for p, j in blocks))
+        return (slice(None), slice(js[0], js[-1] + 1), slice(min(xs), max(xs))), ["@y%d" % j for j in js]
+
+    def keys(kind, J, blocks):
+        return ["%s%d%d%d" % (kind, J, p, j) for p, j in blocks]
+
+    def every(J, axes):
+        return [(p, j) for p in range(len(parts(J))) for j in axes]
+
+    def dots(J, src, rd, ext=()):
+        for j in (2, 0, 1):
             i = (j + 2) % 3
-            mm(Y[j][:, 0:S], T[src][:, 128 * i:128 * i + 128], T.posr[:], True, True, rd + ["posr"], [YK[j]], ext)
+            mm(T.y[:, j, 0:S], T[src][:, 128 * i:128 * i + 128], T.posr[:], True, True, rd + ["posr"], ["@y%d" % j], ext)
 
-    def floor_a(J, j, on):
-        out, sc, bi = T["ga%d" % J][:, S * j:S * j + S], COEF[j] / 2048, COEF[j] * (192 - 511.5 / 2048)
+    def floor_a(J, blocks, on):
+        ix, yk = span(J, blocks)
+        sc, bi = 1.0 / 2048, 192 - 511.5 / 2048
         if on == "a":
-            act(out, Y[j][:, 0:S], AF.Copy, [YK[j]], ["ga%d%d" % (J, j)], bias=bi, scale=sc)
+            act(T["ga%d" % J][ix], T.y[ix], AF.Copy, yk, keys("ga", J, blocks), bias=bi, scale=sc)
         else:
-            ts(out, Y[j][:, 0:S], sc, bi, ALU.mult, ALU.add, [YK[j]], ["ga%d%d" % (J, j)])
+            ts(T["ga%d" % J][ix], T.y[ix], sc, bi, ALU.mult, ALU.add, yk, keys("ga", J, blocks))
 
-    def floor_b(J, j):
-        act(T["gb%d" % J][:, S * j:S * j + S], Y[j][:, 0:S], AF.Copy, [YK[j]], ["gb%d%d" % (J, j)],
-            bias=-COEF[j] * (192 + 512.5 / 2048), scale=-COEF[j] / 2048)
+    def floor_b(J, axes):
+        ix, yk = span(J, every(J, axes))
+        act(T["gb%d" % J][ix], T.y[ix], AF.Copy, yk, keys("gb", J, every(J, axes)), bias=-(192 + 512.5 / 2048), scale=-1.0 / 2048)
 
-    def wrap(J, j, on):
-        out = T["f3%d" % J][:, S * j:S * j + S]
+    def wrap(J, blocks, on):
+        ix, yk = span(J, blocks)
+        out, mod = T["f3%d" % J][ix], MOD[blocks[0][1]]
         if on == "a":
-            act(out, Y[j][:, 0:S], AF.Copy, [YK[j]], ["f3%d%d" % (J, j)],
-                bias=-COEF[j] * (512.5 / 2048 + 191.5 * MOD[j]), scale=-COEF[j] / 2048)
+            act(out, T.y[ix], AF.Copy, yk, keys("f3", J, blocks), bias=-(512.5 / 2048 + 191.5 * mod), scale=-1.0 / 2048)
         else:
-            c = COEF[j] * (192 - MOD[j] * (192 - (MOD[j] - 1) / (2 * MOD[j])))
-            ts(out, T["ga%d" % J][:, S * j:S * j + S], -1.0, c, ALU.mult, ALU.add, ["ga%d%d" % (J, j)], ["f3%d%d" % (J, j)])
+            ts(out, T["ga%d" % J][ix], -1.0, 192 - 192 * mod + (mod - 1) / 2, ALU.mult, ALU.add, keys("ga", J, blocks), keys("f3", J, blocks))
 
-    def place_terms(J, order, which=range(6)):
-        for i in which:
-            kind, j = order[i]
-            mm(T.z[:, 0:S], T.id1[:], T["%s%d" % (kind, J)][:, S * j:S * j + S], i == 0, i == 5, ["id1", "%s%d%d" % (kind, J, j)], ["@z"])
+    def place_terms(J, p, order):
+        x0, x1 = parts(J)[p]
+        for i, (kind, j) in enumerate(order):
+            mm(T.z[:, x0:x1], T[CID[j]][:], T["%s%d" % (kind, J)][:, j, x0:x1], i == 0, i == 5, [CID[j]] + keys(kind, J, [(p, j)]), ["@z"])
 
-    def places(J):
+    def places(J, p):
+        x0, x1 = parts(J)[p]
         c = sum(192 * COEF[j] * (MOD[j] - 1) for j in range(3))
-        ts(T["off%d" % J][:], T.z[:, 0:S], c, None, ALU.add, None, ["@z"], ["off%d" % J])
+        ts(T["off%d" % J][:, x0:x1], T.z[:, x0:x1], c, None, ALU.add, None, ["@z"], ["off%d%d" % (J, p)])
 
-    def score_terms(J, bank, x0, x1, terms, stop=False):
-        for i, (kind, j) in enumerate(terms):
-            mm(T[bank][:, x0:x1], CID[j][0][:], T["%s%d" % (kind, J)][:, S * j + x0:S * j + x1], False, stop and i == len(terms) - 1,
-               [CID[j][1], "%s%d%d" % (kind, J, j)], ["@" + bank])
+    def score_terms(J, kind, axes):
+        for j in axes:
+            mm(bk("s%d" % J), T.id8k[:], T["%s%d" % (kind, J)][:, j, :], False, False, ["id8k"] + keys(kind, J, every(J, [j])), ["@s%d" % J])
 
-    def score_start(J, t, bank, x0, x1, nb):
-        mm(T[bank][:, x0:x1], T.id8k[:], T["live%d" % t][:, x0:x1], True, False, ["id8k", "live%d" % t], ["@" + bank])
-        score_terms(J, bank, x0, x1, [("ga", j) for j in range(3)] + [("gb", j) for j in range(nb)])
+    def score_start(J, t, nb):
+        mm(bk("s%d" % J), T.id8k[:], T["live%d" % t][:], True, False, ["id8k", "live%d" % t], ["@s%d" % J])
+        score_terms(J, "ga", range(3))
+        score_terms(J, "gb", range(nb))
+
+    def verdict(J, name):
+        act(T["nh%d" % J][:], bk("s%d" % J), AF.Sign, ["@s%d" % J, "thc"], ["nh%d" % J, name],
+            bias=T.thc[:, 0:1], scale=-1.0, accum_out=T[name][:, 0:1])
+        send(name, [name])
 
     def pieces(J, names, r=None):
         return ["pr%d%s%d" % (J, x, q) for x in names for q in (range(4) if r is None else [r])]
 
     def gather_a(J, name, x0, x1):
-        act(T["pr%d" % J][:, 16 * x0:16 * x1], T.rfb[:].indirect(T["off%d" % J][:, x0:x1]), AF.Copy, ["off%d" % J], pieces(J, name), RF)
+        act(T["pr%d" % J][:, 16 * x0:16 * x1], T.rfb[:].indirect(T["off%d" % J][:, x0:x1]), AF.Copy,
+            ["off%d%d" % (J, len(parts(J)) - 1)], pieces(J, name), RF)
 
     def gather_v(J, name, x0, x1):
         tt(T["pr%d" % J][:, 16 * x0:16 * x1], T.rfb[:].indirect(T["off%d" % J][:, x0:x1]), T.pfx[:, 16 * (x0 - X0):16 * (x1 - X0)], ALU.mult,
-           ["off%d" % J] + ["pfx%d" % m for m in range(16)], pieces(J, name), RF)
+           ["off%d0" % J] + ["pfx%d" % m for m in range(16)] + (["pfy%d" % m for m in range(16)] if x0 < XH else []), pieces(J, name), RF)
 
-    def times(J, names, r, x0, x1):
-        part = T["pr%d" % J][:, 16 * x0 + r:16 * x1:4]
-        tt(part, part, T.pf4[:, 4 * x0:4 * x1], ALU.mult, pieces(J, names, r) + ["@pf4"], pieces(J, names, r))
+    def times(J, names, r, step, x0, x1):
+        part, k = T["pr%d" % J][:, 16 * x0 + r:16 * x1:step], [p for q in range(r, 4, step) for p in pieces(J, names, q)]
+        tt(part, part, T.pf8[:, 4 * x0:4 * x1:step // 2, :], ALU.mult, k + ["@pf8"], k)
+
+    def turn_profiles():
+        for c in range(NC):
+            op("p", lambda c=c: P.transpose(T.pf8[:, 64 * c:64 * c + 64, :], T.pf2[:, 128 * c:128 * c + 128], T.id1[:]),
+               ["pf20", "pf21", "id1"], ["@pf8"])
+        cp(T.pft[:, 0:128 * NC], T.pf8[:, 0:64 * NC, :], ["@pf8"], ["pft"])
+
+    def turn_back():
+        for c in range(NC):
+            for i in range(4):
+                op("p", lambda c=c, i=i: P.transpose(T.pf8[:, 256 * c + i:256 * c + 256:4, :], T.pft[:, 128 * c:128 * c + 128], T.id1[:]),
+                   ["pft", "id1"], ["@pf8"])
 
     def sums(J, names, r, bank, x0, x1, stop=True):
-        for i in range(4):
-            m = r + 4 * i
-            mm(T[bank][:, x0:x1], T.wd[:, 15 - m:143 - m], T["pr%d" % J][:, 16 * x0 + m:16 * x1:16], False, stop and r == 3 and i == 3,
+        for m in range(r, 16, 4):
+            mm(bk(bank)[:, x0:x1], T.wd[:, 15 - m:143 - m], T["pr%d" % J][:, 16 * x0 + m:16 * x1:16], False, stop and m == 15,
                ["wd"] + pieces(J, names, r), ["@" + bank])
 
-    def verdict(J, bank, x0, x1, out, key):
-        act(T["nh%d" % J][:, x0:x1], T[bank][:, x0:x1], AF.Sign, ["@" + bank, "thc"], ["nh" + key, key],
-            bias=T.thc[:, 0:1], scale=-1.0, accum_out=out)
-
     def winner_early(J, one, ext=()):
-        rd = [] if ext else [one]
-        ts(T["tot%d" % J][:, 0:1], T[one][:, 0:1], T.col[:, 3:4], None, ALU.add, None, rd + ["col3"], ["tot%da" % J], ext)
-        ts(T["pk%d" % J][:], T.pen32[:], T["tot%d" % J][:, 0:1], None, ALU.add, None,
-           ["pen32%d" % q for q in range(0, 128, 32)] + ["tot%da" % J], ["pk%d" % J])
+        ts(T.tot[:, J:J + 1], T[one][:, 0:1], T.col[:, 3:4], None, ALU.add, None, ["col3"] + ([] if ext else [one]), ["tot%d" % J], ext)
 
-    def winner(J, two, rd, ext=()):
-        a, b = T[two][:, 0:1], T[two][:, 1:2]
-        tot = T["tot%d" % J][:, 1:2]
-        ts(T.k32[:], T["pk%d" % J][:], a, b, ALU.add, ALU.add, ["pk%d" % J] + rd, ["k32"], ext)
-        ts(tot, T["tot%d" % J][:, 0:1], a, b, ALU.add, ALU.add, ["tot%da" % J] + rd, ["tot%db" % J])
-        op("v", lambda: V.transpose(T.k32t[:], T.k32[:]), ["k32"], ["k32t"])
+    def winner(J, late, rd, pen, win, ext=()):
+        key = "key%d" % J
+        ts(T[key][:], T.pen32[:], T.tot[:, J:J + 1], late, ALU.add, ALU.add,
+           ["pen32%d" % q for q in range(0, 129, 32)] + ["tot%d" % J] + rd, [key], ext)
+        op("v", lambda: V.transpose(T.k32t[:], T[key][:, 1:33]), [key], ["k32t"])
         op("v", lambda: V.tensor_reduce(T.mn[:, 0:1], T.k32t[:], AX.X, ALU.min), ["k32t"], ["mn"])
-        ts(T["win%d" % J][:], T.pen[:], tot, T.mn[:, 0:1], ALU.add, ALU.is_le, ["pen", "mn", "tot%db" % J], ["win%d" % J])
+        ts(T[win][:], T[pen][:], T[key][:, 0:1], T.mn[:, 0:1], ALU.add, ALU.is_le, [pen, "mn", key], [win])
+
+    def limits():
+        ts(T.thb[:, 0:1], T.thc[:, 0:1], -1.0, 3 * BIG, ALU.mult, ALU.add, ["thc"], ["thb0"])
+        ts(T.col[:, 5:6], T.thc[:, 0:1], -1.0, 3 * BIG, ALU.mult, ALU.add, ["thc"], ["col5"])
+
+    def limits_end():
+        ts(T.col[:, 6:7], T.col[:, 5:6], T.thb[:, 0:1], None, ALU.subtract, None, ["col5", "thb0"], ["col6"])
+        for i in range(2):
+            ts(T.thd[:, 128 * i:128 * i + 128], T.id1[:], T.col[:, 5 + i:6 + i], None, ALU.mult, None, ["id1", "col%d" % (5 + i)], ["thd%d" % i])
+
+    def turned(c):
+        return (T.s1, "@s1") if c else (T.z, "@z")
+
+    def turned_terms(c, nb):
+        bank, key = turned(c)
+        x, live = slice(128 * c, 128 * c + 128), "live%d" % now[0]
+        for i in range(2):
+            mm(bank[:, x], T[live][:, x], T.thd[:, 128 * i:128 * i + 128], i == 0 and c != 1, False, [live, "thd%d" % i], [key])
+        for kind, j in [("ga", j) for j in range(3)] + [("gb", j) for j in range(nb)]:
+            mm(bank[:, x], T[kind + "1"][:, j, x], T.id8k[:], False, False, ["id8k"] + keys(kind, 1, [(0, j)]), [key])
+
+    def turned_late(nb):
+        for c in (2, 1, 0):
+            bank, key = turned(c)
+            for j in range(nb, 3):
+                mm(bank[:, 128 * c:128 * c + 128], T.gb1[:, j, 128 * c:128 * c + 128], T.id8k[:], False, False,
+                   ["id8k"] + keys("gb", 1, [(0, j)]), [key])
+
+    def turned_sums(names, c, residues):
+        bank, key = turned(c)
+        for r in residues:
+            for m in range(r, 16, 4):
+                mm(bank[:, 128 * c + m:128 * c + 128:16], T.pr1[:, 2048 * c + m:2048 * c + 2048:16], T.blk[:, 8:16], False, m == 15 and c < 2,
+                   ["blk1"] + pieces(1, names, r), [key])
+
+    def turned_verdict(chunks):
+        bank, key = turned(chunks[0])
+        x = slice(128 * chunks[0], 128 * chunks[-1] + 128)
+        act(T.nt[:, x], bank[:, x], AF.Sign, [key], ["nt%d" % chunks[0]], bias=2 * BIG, scale=-1.0)
+
+    def turned_back(chunks):
+        k = "nt%d" % chunks[0]
+        for c in chunks:
+            mm(T.y[:, 0, 0:1], T.nt[:, 128 * c:128 * c + 128], T.one[:, 0:1], c == 1, c == 0, [k, "one"], ["@y0"])
+        for c in chunks:
+            mm(T.y[:, 1, 128 * c:128 * c + 128], T.nt[:, 128 * c:128 * c + 128], T.id1[:], True, True, [k, "id1"], ["@y1"])
+        if chunks[0] == 0:
+            act(T.nh1[:], bk("y1"), AF.Copy, ["@y1"], ["nh1"])
+
+    def all_sums(J, names, x0, x1, stop=False):
+        for r in range(4):
+            sums(J, names, r, "s%d" % J, x0, x1, stop)
+
+    def other_places():
+        wrap(1, every(1, [0, 1]), "a")
+        wrap(1, every(1, [2]), "a")
+        place_terms(1, 0, [(k, j) for k in ("ga", "f3") for j in range(3)])
+
+    def opening(J, ax, nb, first):
+        dots(J, ax, [ax])
+        floor_a(J, [(0, 2)], "v")
+        floor_a(J, [(0, 0)], "a")
+        floor_a(J, [(0, 1)], "a")
+        wrap(J, [(0, 2)], "v")
+        wrap(J, [(0, 0)], "v")
+        wrap(J, [(0, 1)], "v")
+        place_terms(J, 0, [("ga", 2), ("ga", 0), ("f3", 2), ("f3", 0), ("ga", 1), ("f3", 1)])
+        floor_a(J, [(1, 2)], "v")
+        if first:
+            pfx_copies("a1")
+        floor_a(J, [(1, 0), (1, 1)], "a")
+        if first:
+            pfx_copies("v1")
+        wrap(J, [(1, 0), (1, 1)], "a")
+        places(J, 0)
+        wrap(J, [(1, 2)], "v")
+        place_terms(J, 1, [("ga", 2), ("f3", 2), ("ga", 0), ("ga", 1), ("f3", 0), ("f3", 1)])
+        if first:
+            ts(T.id8k[:], T.uu[:], 0.0, BIG, ALU.is_equal, ALU.mult, ["uu"], ["id8k"])
+        gather_v(J, "u", U, S)
+        if first:
+            flags(0)
+        floor_b(J, range(nb))
+        places(J, 1)
 
     pfx_copies("g0")
     early_b = 3 - LATE_B
@@ -415,100 +565,106 @@ def rank_program(g, core, T, topo):
             pfx_copies("g1")
             pool_constants()
             pfx_copies("a0")
-            ts(T.id1[:], T.uu[:], 0.0, None, ALU.is_equal, None, ["uu"], ["id1"])
-            ts(T.pc2[:, 0:1], T.pci[:, 0:1], 15, None, ALU.bitwise_and, None, ["pci"], ["m"])
-            ts(T.thc[:, 0:1], T.thi[:, 0:1], BIG - 0.5, None, ALU.add, None, [], ["thc"], TH)
-            ts(T.col[:, 3:4], T.pc2[:, 0:1], 1.0 / 32, None, ALU.mult, None, ["m"], ["col3"])
-            ts(T.col[:, 4:5], T.pc2[:, 0:1], -1.0 / 32, -2.0 * S, ALU.mult, ALU.add, ["m"], ["col4"])
+            for j in (2, 0, 1):
+                ts(T[CID[j]][:], T.uu[:], 0.0, COEF[j], ALU.is_equal, ALU.mult, ["uu"], [CID[j]])
             pfx_copies("v0")
         else:
             lattices(t, T.win0[:], 128, "surv")
-        dots("ax%d" % t, ["ax%d" % t])
-        floor_a(0, 0, "a")
-        floor_a(0, 1, "a")
-        floor_a(0, 2, "v")
-        wrap(0, 0, "v")
-        wrap(0, 2, "v")
-        wrap(0, 1, "v")
-        place_terms(0, [("ga", 0), ("ga", 2), ("f3", 0), ("ga", 1), ("f3", 2), ("f3", 1)])
+        now[0] = t
+        (xa0, xa1), ga, f0, f1, last = XA[t], GA, F0[t], F1, L[t]
+        opening(0, "ax0", 3, t == 0)
         if t == 0:
-            pfx_copies("a1")
-            pfx_copies("v1")
-        for j in range(3):
-            floor_b(0, j)
-        if t == 0:
-            for x0 in range(0, max(XA), 128):
-                x1 = min(x0 + 128, max(XA))
-                for i in range(4):
-                    mm(T.pf4[:, 4 * x0 + i:4 * x1:4], T.id1[:], T.pfb[:, x0:x1], True, True, ["id1"], ["@pf4"], PFD)
-        places(0)
-        gather_a(0, "a", 0, XA[0])
-        gather_v(0, "v", XA[0], S)
-        dots("rt%d" % t, [], came("rt%d" % t))
-        score_start(0, t, "s0", 0, S, 3)
-        for j in range(3):
-            floor_a(1, j, "a")
-            wrap(1, j, "a")
-        order = [(k, j) for j in range(3) for k in ("ga", "f3")]
+            gather_a(0, "a", 0, xa0)
+            ts(T.thc[:, 0:1], T.thi[:, 0:1], BIG - 0.5, None, ALU.add, None, [], ["thc"], TH)
+            limits()
+            turn_profiles()
+            gather_v(0, "v", f0, U)
+            score_start(0, t, 3)
+            turn_back()
+            spread("ax1", "rt0", [], came("rt0"))
+            gather_v(0, "w", xa0, f0)
+            dots(1, "ax1", ["ax1"])
+            all_sums(0, "uv", f0, S)
+            floor_a(1, every(1, range(3)), "a")
+            other_places()
+            floor_b(1, range(early_b))
+            for r in range(2):
+                times(0, "a", r, 2, 0, xa0)
+            limits_end()
+            columns()
+            places(1, 0)
+            all_sums(0, "aw", 0, f0, True)
+            gather_v(1, "uv", 256, S)
+            for c in (2, 1, 0):
+                turned_terms(c, early_b)
+        else:
+            score_start(0, t, 0)
+            gather_a(0, "a", 0, ga)
+            gather_v(0, "v", f0, U)
+            dots(1, "rt1", [], came("rt1"))
+            score_terms(0, "gb", range(3))
+            floor_a(1, every(1, range(3)), "a")
+            other_places()
+            places(1, 0)
+            gather_a(0, "b", ga, xa0)
+            gather_v(0, "w", xa0, f0)
+            all_sums(0, "uv", f0, S)
+            floor_b(1, range(early_b))
+            gather_v(1, "u", f1, S)
+            for r in range(2):
+                times(0, "ab", r, 2, 0, xa0)
+            turned_terms(2, early_b)
+            all_sums(0, "abw", 0, f0, True)
+            turned_terms(1, early_b)
+            turned_terms(0, early_b)
+            gather_v(1, "v", 256, f1)
+        gather_a(1, "b", last, xa1)
+        verdict(0, so)
+        if LATE_B:
+            floor_b(1, range(early_b, 3))
+        gather_a(1, "c", 0, last)
+        turned_sums("uv", 2, range(4))
+        gather_v(1, "x", xa1, 256)
+        turned_late(early_b)
+        for r in range(2):
+            times(1, "b", r, 2, last, xa1)
+            turned_sums("bx", 1, (r, r + 2))
+        turned_verdict((1, 2))
         for r in range(4):
-            times(0, "a", r, 0, XA[0])
-            sums(0, "v", r, "s0", XA[0], S, False)
-            if r < 3:
-                place_terms(1, order, (2 * r, 2 * r + 1))
-        places(1)
-        for r in range(4):
-            sums(0, "a", r, "s0", 0, XA[0])
-        for j in range(early_b):
-            floor_b(1, j)
-        gather_v(1, "v", XA[1], S)
-        gather_a(1, "a", L1, XA[1])
-        verdict(0, "s0", 0, S, T[so][:, 0:1], so)
-        send(so, [so])
-        gather_a(1, "b", L, L1)
-        gather_a(1, "c", 0, L)
-        score_start(1, t, "s1", L, S, early_b)
-        score_start(1, t, "z", 0, L, early_b)
-        mm(T.s0[:, 0:S], T.id8k[:], T[live][:], True, False, ["id8k", live], ["@s0"])
-        mm(T.s0[:, 0:S], T.id1[:], T.nh0[:], False, False, ["id1", "nh" + so], ["@s0"])
-        for r in range(4):
-            sums(1, "v", r, "s1", XA[1], S, False)
-        for r in range(4):
-            times(1, "a", r, L1, XA[1])
-            sums(1, "a", r, "s1", L1, XA[1], False)
-        for r in range(4):
-            times(1, "b", r, L, L1)
-            sums(1, "b", r, "s1", L, L1, LATE_B == 0)
+            times(1, "c", r, 4, 0, last)
+            turned_sums("bc", 0, [r])
+        turned_back((1, 2))
         winner_early(0, so)
-        late = [("gb", j) for j in range(early_b, 3)]
-        for j in range(early_b, 3):
-            floor_b(1, j)
-        for r in range(4):
-            times(1, "c", r, 0, L)
-            if r == 2:
-                score_terms(1, "s1", L, S, late, True)
-                score_terms(1, "z", 0, L, late)
-            sums(1, "c", r, "z", 0, L)
-        verdict(1, "s1", L, S, T[sf][:, 0:1], sf + "a")
-        verdict(1, "z", 0, L, T[sf][:, 1:2], sf + "b")
-        send(sf, [sf + "a", sf + "b"])
+        turned_verdict((0,))
+        turned_back((0,))
+        cp(T[sf][:, 0:1], T.y[:, 0, 0:1], ["@y0"], [sf])
+        send(sf, [sf])
+        winner_early(1, ra, came(ra))
+        mm(T.s0[:, 0:S], T.id8k[:], T[live][:], True, False, ["id8k", live], ["@s0"])
+        mm(T.s0[:, 0:S], T.id1[:], T.nh0[:], False, False, ["id1", "nh0"], ["@s0"])
+        Q = S // 4
         if t < RO - 1:
-            thresholds(t + 1)
+            thresholds(t + 1, range(3))
         else:
             for u in range(RO):
-                mm(T.y0[0:8, 0:S], T.id1[:, ::16], T["live%d" % u][:], u == 0, False, ["id1", "live%d" % u], ["@y0"])
-        winner_early(1, ra, came(ra))
-        winner(1, sf, [sf + "a", sf + "b"])
-        mm(T.s0[:, 0:S], T.win1[:], T.nh1[:], False, True, ["win1", "nh" + sf + "a", "nh" + sf + "b"], ["@s0"])
-        ts(T.surv[:], T.s0[:, 0:S], BIG + 1.5, None, ALU.is_ge, None, ["@s0"], ["surv"])
+                for q in range(4):
+                    mm(T.y[0:32, 0, 0:Q], T.sel4[:, 32 * q:32 * q + 32], T["live%d" % u][:, Q * q:Q * q + Q], u + q == 0, False,
+                       ["sel4", "live%d" % u], ["@y0"])
+        winner(1, T[sf][:, 0:1], [sf], "pen", "win1")
+        mm(T.s0[:, 0:S], T.win1[:], T.nh1[:], False, True, ["win1", "nh1"], ["@s0"])
         if t < RO - 1:
+            ts(T.surv[:], T.s0[:, 0:S], BIG + 1.5, None, ALU.is_ge, None, ["@s0"], ["surv"])
             scan(T.cum[:], T.surv[:], T.surv[:], ALU.add, ALU.max, ["surv"], ["cum"])
-        winner(0, rb, [], came(rb))
-        if t == RO - 1:
-            mm(T.y0[0:8, 0:S], T.win0[:, ::16], T.surv[:], False, True, ["win0", "surv"], ["@y0"])
-        ts(T.ycs[:, t:t + 1], T.tot0[:, 1:2], T.col[:, 4:5], -0.5, ALU.add, ALU.mult, ["tot0b", "col4"], ["ycs%d" % t])
-    cp(T.yas[0:8, :], T.y0[0:8, 0:S], ["@y0"], ["yas"])
+            winner(0, T[rb][:, 0:1], [], "pen", "win0", came(rb))
+        else:
+            act(T.junk[:], T.s0[:, 0:S], AF.Relu, ["@s0"], ["junk"], bias=-BIG - 1)
+            winner(0, T[rb][:, 0:1], [], "pen4", "win4", came(rb))
+            for q in range(4):
+                mm(T.y[0:32, 0, 0:Q], T.win4[:, 32 * q:32 * q + 32], T.junk[:, Q * q:Q * q + Q], False, q == 3, ["win4", "junk"], ["@y0"])
+        ts(T.ycs[:, t:t + 1], T.key0[:, 0:1], T.col[:, 4:5], -0.5, ALU.add, ALU.mult, ["key0", "col4"], ["ycs%d" % t])
+    cp(T.yas[0:32, :], T.y[0:32, 0, 0:Q], ["@y0"], ["yas"])
     op("a", lambda: g.scalar.dma_start(T.yc[:], T.ycs[:, 0:RO]).then_inc(T.sem.d_out, 16), ["ycs%d" % t for t in range(RO)], [])
-    op("s", lambda: g.sync.dma_start(T.ya[:], T.yas[0:8, :]).then_inc(T.sem.d_out, 16), ["yas"], [])
+    op("s", lambda: g.sync.dma_start(T.ya[:], T.yas[0:32, :]).then_inc(T.sem.d_out, 16), ["yas"], [])
     emit(ops, {"v": V, "a": A, "p": P, "g": g, "s": g.sync}, T)
     g.sync.wait_ge(T.sem.d_out, 32)
     g.wait_ge(T.sem.sent, sent[0])

from concourse.mybir import AluOpType as ALU, AxisListType as AX, ActivationFunctionType as AF

S = 384
RO = 2
XA = [[160, 192], [150, 192]]
XH, X0 = XA[0][0], min(XA[0] + XA[1])
XD = S - X0
U = 360
F0 = [250, 180]
F1 = 330
GA = 56
L = [84, 64]
LATE_B = 1
AXES = ["gs0", "ax0"]
COEF = [128.0, 8.0, 1.0]
MOD = [16.0, 16.0, 8.0]
BIG = 8192.0
WB = S + 1
COPIES = {"g0": 3, "g1": 2, "a0": 4, "a1": 1, "v0": 3, "v1": 3}

SCRATCH = {
    "posb": ("sbuf", [128, S], "bfloat16"), "tb": ("sbuf", [128, S], "bfloat16"),
    "lvi": ("sbuf", [128, S], "int32"), "lvb": ("sbuf", [128, S], "float16"),
    "pfb": ("sbuf", [128, S], "bfloat16"), "rfb": ("sbuf", [128, 2048], "bfloat16"),
    "thi": ("sbuf", [128, 8], "int32"), "thc": ("sbuf", [128, 8], "float32"),
    "w": ("sbuf", [128, 2 * WB], "bfloat16"), "posr": ("sbuf", [128, S], "bfloat16"),
    "pfx": ("sbuf", [128, 16 * XD], "bfloat16"),
    "qp": ("sbuf", [128, 96], "bfloat16"), "qm": ("sbuf", [128, 96], "bfloat16"), "sel": ("sbuf", [128, 384], "bfloat16"),
    "sgn": ("sbuf", [128, 128], "bfloat16"), "sb1": ("sbuf", [128, 128], "bfloat16"), "sb2": ("sbuf", [128, 128], "bfloat16"),
    "pci": ("sbuf", [128, 8], "int32"), "pc2": ("sbuf", [128, 8], "int32"),
    "sel4": ("sbuf", [128, 128], "bfloat16"), "pen4": ("sbuf", [128, 128], "bfloat16"), "win4": ("sbuf", [128, 128], "bfloat16"),
    "col": ("sbuf", [128, 8], "float32"), "k2": ("sbuf", [128, 8], "float32"), "blk": ("sbuf", [128, 16], "bfloat16"),
    "uu": ("sbuf", [128, 128], "bfloat16"), "u2": ("sbuf", [128, 128], "bfloat16"), "zero": ("sbuf", [128, 128], "bfloat16"),
    "pen1": ("sbuf", [128, 128], "bfloat16"),
    "offe": ("sbuf", [128, 8], "uint16"), "thr": ("sbuf", [128, 128], "bfloat16"),
    "cst": ("sbuf", [128, S], "bfloat16"), "ramp": ("sbuf", [128, S], "float16"),
    "sell": ("sbuf", [128, 128], "float16"), "wd": ("sbuf", [128, 144], "bfloat16"),
    "id1": ("sbuf", [128, 128], "bfloat16"), "id8k": ("sbuf", [128, 128], "bfloat16"),
    "id128": ("sbuf", [128, 128], "bfloat16"), "id8": ("sbuf", [128, 128], "bfloat16"),
    "thb": ("sbuf", [128, 8], "bfloat16"), "thd": ("sbuf", [128, 256], "bfloat16"), "nt": ("sbuf", [128, S], "bfloat16"),
    "nh0": ("sbuf", [128, S], "bfloat16"), "nh1": ("sbuf", [128, S], "bfloat16"),
    "one": ("sbuf", [128, 8], "bfloat16"), "tot": ("sbuf", [128, 8], "float32"), "pen32": ("sbuf", [128, 33], "bfloat16"), "pen": ("sbuf", [128, 128], "bfloat16"),
    "cum": ("sbuf", [128, S], "float16"), "junk": ("sbuf", [128, S], "bfloat16"), "sc": ("sbuf", [128, 2 * S], "float16"),
    "cnt": ("sbuf", [128, 8], "float32"), "offs": ("sbuf", [128, 8], "uint16"),
    "live0": ("sbuf", [128, S], "bfloat16"), "live1": ("sbuf", [128, S], "bfloat16"), "surv": ("sbuf", [128, S], "float16"),
    "key0": ("sbuf", [128, 33], "float32"), "key1": ("sbuf", [128, 33], "float32"), "k32t": ("sbuf", [128, 32], "float32"),
    "mn": ("sbuf", [128, 8], "float32"), "win0": ("sbuf", [128, 128], "float16"), "win1": ("sbuf", [128, 128], "bfloat16"),
    "ycs": ("sbuf", [128, 8], "float32"), "yas": ("sbuf", [128, S // 4], "float32"),
    "y": ("psum", [128, 3, 512], "float32"),
    "z": ("psum", [128, 512], "float32"), "s0": ("psum", [128, 512], "float32"), "s1": ("psum", [128, 512], "float32"),
    "pf8": ("psum", [128, 1024, 2], "bfloat16"), "pf2": ("sbuf", [128, 512], "bfloat16"), "pft": ("sbuf", [128, 512], "bfloat16"),
}
for _j in range(2):
    SCRATCH["ga%d" % _j] = ("sbuf", [128, 3, S], "bfloat16")
    SCRATCH["gb%d" % _j] = ("sbuf", [128, 3, S], "bfloat16")
    SCRATCH["f3%d" % _j] = ("sbuf", [128, 3, S], "bfloat16")
    SCRATCH["ax%d" % _j] = ("sbuf", [128, 384], "bfloat16")
    SCRATCH["off%d" % _j] = ("sbuf", [128, S], "uint16")
    SCRATCH["pr%d" % _j] = ("sbuf", [128, 16 * S], "bfloat16")
for _t in range(RO):
    SCRATCH["gs%d" % _t] = ("sbuf", [128, 96], "bfloat16")
    SCRATCH["rt%d" % _t] = ("sbuf", [128, 384], "bfloat16")
    SCRATCH["so%d" % _t] = ("sbuf", [128, 8], "float32")
    SCRATCH["sf%d" % _t] = ("sbuf", [128, 8], "float32")
    SCRATCH["ra%d" % _t] = ("sbuf", [128, 8], "float32")
    SCRATCH["rb%d" % _t] = ("sbuf", [128, 8], "float32")

SEMAPHORES = ["v", "a", "p", "g", "sent", "d_lv", "d_pos", "d_pf", "d_th", "d_rf", "d_out"]
for _t in range(RO):
    SEMAPHORES += ["rt%d" % _t, "ra%d" % _t, "rb%d" % _t]


def bits(m):
    return bin(m).count("1")


def relay_of(src, dsts, T, topo):
    ok = [c for c in topo.cores_of(src) if T.rank_of(c) is None and all(topo.may_write(c, d) for d in dsts)]
    near = [c for c in ok if topo.die(c) == topo.die(src)]
    return (near or ok)[0]


def routes(rank, T, topo):
    n = len(T.cores)
    src = T.cores[rank]
    msgs = []
    for t in range(RO):
        nxt, prv = T.cores[(rank + t + 1) % n], T.cores[(rank - t - 1) % n]
        msgs += [(AXES[t], "rt%d" % t, 96 if AXES[t][0] == "g" else 384, nxt), ("so%d" % t, "ra%d" % t, 1, nxt), ("sf%d" % t, "rb%d" % t, 1, prv)]
    barred = [m[3] for m in msgs if not topo.may_write(src, m[3])]
    via = relay_of(src, barred, T, topo) if barred else None
    return [m + ((None if topo.may_write(src, m[3]) else via),) for m in msgs]


def mask_of(topo, src, dst, name):
    e = topo.engines(src, dst)
    if name == "rt0" and dst in topo.cores_of(src):
        e = e[:len(e) // 2]
    return sum(1 << x for x in e)


def remote(g, T, topo, src, dst, out_name, in_name, cols):
    rid, pid = topo.addr(dst, src)
    m = mask_of(topo, src, dst, out_name)
    g.remote_dma(T[out_name][:, 0:cols], T[in_name][:, 0:cols], T.sem[out_name], T.sem.sent, pid, rid, m)
    return bits(m)


def relay_program(g, core, T, topo):
    total = 0
    for r in range(len(T.cores)):
        for (_, far, cols, dst, via) in routes(r, T, topo):
            if via == core:
                g.wait_ge(T.sem[far], bits(mask_of(topo, T.cores[r], core, far)))
                total += remote(g, T, topo, core, dst, far, far, cols)
    if total:
        g.wait_ge(T.sem.sent, total)


def emit(ops, queues, T):
    writer, readers, deps = {}, {}, []
    for i, (q, fn, rd, wr, ext) in enumerate(ops):
        d = set()
        for k in rd:
            if k in writer and (k[0] == "!" or not (q == "p" and ops[writer[k]][0] == "p")):
                d.add(writer[k])
            if k[0] == "@":
                d.update(j for j in readers.get(k, []) if ops[j][0] != q)
        for k in wr:
            if k in writer and not (q == "p" and ops[writer[k]][0] == "p"):
                d.add(writer[k])
            d.update(readers.get(k, []))
        for k in rd:
            readers.setdefault(k, []).append(i)
        for k in wr:
            writer[k] = i
            readers[k] = []
        d.discard(i)
        deps.append(d)
    need = []
    for i, d in enumerate(deps):
        last = {}
        for j in d:
            last[ops[j][0]] = max(last.get(ops[j][0], -1), j)
        need.append(last)
    known, snap, marked = {}, [], set()
    for i, last in enumerate(need):
        kq = known.setdefault(ops[i][0], {})
        for e, j in sorted(last.items(), key=lambda x: -x[1]):
            if kq.get(e, -1) >= j:
                del last[e]
            else:
                marked.add(j)
                kq[e] = j
                for e2, j2 in snap[j].items():
                    kq[e2] = max(kq.get(e2, -1), j2)
        snap.append(dict(kq))
    count, number, extseen = {}, {}, set()
    for i, (q, fn, rd, wr, ext) in enumerate(ops):
        for (name, val) in ext:
            if (q, name) not in extseen:
                extseen.add((q, name))
                queues[q].wait_ge(T.sem[name], val)
        for e, j in need[i].items():
            queues[q].wait_ge(T.sem[e], number[j])
        ins = fn()
        if i in marked:
            count[q] = count.get(q, 0) + 1
            number[i] = count[q]
            ins.then_inc(T.sem[q], 1)


def rank_program(g, core, T, topo):
    rank = T.rank_of(core)
    if rank is None:
        relay_program(g, core, T, topo)
        return
    n = len(T.cores)
    V, A, P = g.vector, g.scalar, g.tensor
    ops = []
    arrive = {}
    for r in range(n):
        for (_, far, cols, dst, via) in routes(r, T, topo):
            if dst == core:
                arrive[far] = bits(topo.mask(T.cores[r] if via is None else via, core))
    mine = {m[0]: m for m in routes(rank, T, topo)}
    sent = [0]

    def op(q, fn, rd=(), wr=(), ext=()):
        ops.append((q, fn, list(rd), list(wr), list(ext)))

    def ts(out, in0, s1, s2, op0, op1, rd, wr, ext=()):
        if op1 is None:
            op("v", lambda: V.tensor_scalar(out, in0, s1, None, op0), rd, wr, ext)
        else:
            op("v", lambda: V.tensor_scalar(out, in0, s1, s2, op0, op1), rd, wr, ext)

    def tt(out, a, b, o, rd, wr, ext=()):
        op("v", lambda: V.tensor_tensor(out, a, b, o), rd, wr, ext)

    def cp(out, a, rd, wr, ext=()):
        op("v", lambda: V.tensor_copy(out, a), rd, wr, ext)

    def ms(out, c, wr):
        op("v", lambda: V.memset(out, c), [], wr)

    def scan(out, d0, d1, op0, op1, rd, wr):
        op("v", lambda: V.tensor_tensor_scan(out, d0, d1, 0.0, op0, op1), rd, wr)

    def act(out, a, f, rd, wr, ext=(), **kw):
        op("a", lambda: A.activation(out, a, f, **kw), rd, wr, ext)

    def mm(out, l, r, st, sp, rd, wr, ext=()):
        op("p", lambda: P.matmul(out, l, r, st, sp), rd, wr, ext)

    def iota(out, pat, base, cm, wr, f=True):
        if f:
            op("g", lambda: g.iota(out, pat, base, cm, allow_small_or_imprecise_dtypes=True), [], wr)
        else:
            op("g", lambda: g.iota(out, pat, base, cm), [], wr)

    def send(name, rd):
        _, far, cols, dst, via = mine[name]

        def fn():
            sent[0] += remote(g, T, topo, core, dst if via is None else via, far, name, cols)
        op("g", fn, rd, [])

    def came(name):
        return [(name, arrive[name])]

    def bk(name):
        return T.y[:, int(name[1]), 0:S] if name[0] == "y" else T[name][:, 0:S]

    CID = ["id128", "id8", "id1"]

    g.sync.dma_start(T.lvi[0:8, :], T.lv[:]).then_inc(T.sem.d_lv, 16)
    g.scalar.dma_start(T.posb[0:24, :], T.pos[:]).then_inc(T.sem.d_pos, 16)
    g.sync.dma_start(T.pfb[:], T.pf[:]).then_inc(T.sem.d_pf, 16)
    g.scalar.dma_start(T.rfb[:, 0:2048], T.rf[:]).then_inc(T.sem.d_rf, 16)
    g.sync.dma_start(T.thi[:, 0:1], T.th[:]).then_inc(T.sem.d_th, 16)
    LV, POS, PFD, TH, RF = [("d_lv", 16)], [("d_pos", 16)], [("d_pf", 16)], [("d_th", 16)], [("d_rf", 16)]

    COUNT = [("s0", "z", "s1", "s0"), ("y0", "y2", "y1", "s1")]

    def thresholds(t, which):
        for i in which:
            bank, r = COUNT[t][i], (0, 2, 1)[i]
            mm(bk(bank), T.thr[32 * r:32 * r + 1, :], T.cst[32 * r:32 * r + 1, :], True, False, ["thr", "cst"], ["@" + bank, "!" + bank])

    iota(T.qp[0:24, 0:48], [[-1, 3], [-3, 8], [0, 2]], 0, 1, ["qp0"])
    iota(T.qm[0:24, 0:48], [[1, 3], [-3, 8], [0, 2]], -2, 1, ["qm0"])
    iota(T.sgn[0:32, :], [[0, 8], [-2, 2], [0, 8]], 1, 0, ["sgn"])
    iota(T.thr[0:96, :], [[0, 8], [3072, 16]], 512, 32, ["thr"])
    iota(T.u2[0:8, :], [[-1, 8], [0, 16]], 0, 1, ["u2"])
    iota(T.pci[:, 0:4], [[128, 4]], 0, 1, ["pci"], False)
    iota(T.k2[:, 0:2], [[2 * WB, 2]], S, 0, ["k2"])
    iota(T.uu[:], [[-1, 128]], 0, 1, ["uu"])
    ms(T.cst[:], -1.0 / 1024, ["cst"])
    ms(T.sel[0:32, 128:256], -192.0, ["sel"])
    cp(T.qp[0:24, 48:96], T.qp[0:24, 0:48], ["qp0"], ["qp1"])
    for c in (6, 7):
        act(T.sel[0:24, c::8], T.cst[0:24, 0:48], AF.Copy, ["cst", "sel"], ["sel%d" % c], scale=0.0)
    cp(T.qm[0:24, 48:96], T.qm[0:24, 0:48], ["qm0"], ["qm1"])
    for c in range(3):
        ts(T.sel[0:24, c::8], T.qp[0:24, 16 * c:16 * c + 48], 0.0, None, ALU.is_equal, None, ["qp0", "qp1", "sel"], ["sel%d" % c])
    for c in range(3):
        ts(T.sel[0:24, 3 + c:256:8], T.qm[0:24, 32 - 16 * c:64 - 16 * c], 0.0, None, ALU.is_equal, None, ["qm0", "qm1", "sel"], ["sel%d" % (3 + c)])
    SELK = ["sel%d" % r for r in range(8)]
    tt(T.sb2[0:32, :], T.sel[0:32, 128:256], T.sgn[0:32, :], ALU.mult, SELK + ["sgn"], ["sb2"])
    act(T.tb[0:32, :], T.cst[0:32, :], AF.Copy, ["cst"], ["tb"], scale=0.0, bias=1.0)
    act(T.w[:, S::WB], T.cst[:, 0:2], AF.Copy, ["cst"], ["wz"], scale=0.0)
    act(T.ax0[:], T.cst[:], AF.Copy, ["cst"], ["ax0"], scale=0.0)
    act(T.tb[0:24, :], T.posb[0:24, :], AF.Copy, [], ["tb"], POS, bias=1536.0)
    cp(T.lvb[0:8, :], T.lvi[0:8, :], [], ["lvb"], LV)
    ts(T.sb1[0:24, :], T.sb2[0:24, :], -1.0, 0.0, ALU.mult, ALU.max, ["sb2"], ["sb1"])
    scan(T.cum[0:8, :], T.lvb[0:8, :], T.lvb[0:8, :], ALU.add, ALU.max, ["lvb"], ["cum"])
    ts(T.sell[0:8, :], T.u2[0:8, :], 0.0, None, ALU.is_equal, None, ["u2"], ["sell"])
    scan(T.ramp[:], T.cst[:], T.cst[:], ALU.add, ALU.min, ["cst"], ["ramp"])
    for c in range(3):
        ts(T.sel[0:24, 259 + c::8], T.qm[0:24, 64 - 16 * c:80 - 16 * c], 0.0, -1.0, ALU.is_equal, ALU.mult, ["qm0", "qm1"], ["selr%d" % c])

    def columns():
        ts(T.col[:, 3:4], T.pc2[:, 0:1], 1.0 / 32, None, ALU.mult, None, ["m"], ["col3"])
        ts(T.col[:, 4:5], T.pc2[:, 0:1], -1.0 / 32, -2.0 * S, ALU.mult, ALU.add, ["m"], ["col4"])

    thresholds(0, [0])
    mm(bk("y0"), T.sel[0:24, 0:128], T.posb[0:24, :], True, True, SELK, ["@y0"], POS)
    thresholds(0, [1, 2])
    mm(bk("y1"), T.sb2[0:32, :], T.tb[0:32, :], True, False, ["sb2", "tb"], ["@y1"])
    mm(bk("y1"), T.sb1[0:24, :], T.posb[0:24, :], False, True, ["sb1"], ["@y1"])
    act(T.w[:, 0:S], bk("y0"), AF.Copy, ["@y0"], ["wa"])
    act(T.w[:, WB:WB + S], bk("y1"), AF.Copy, ["@y1"], ["wb"])

    todo = list(range(16))

    def pfx_copies(who):
        for _ in range(COPIES[who]):
            m = todo.pop()
            out, src = T.pfx[:, 16 * (XH - X0) + m::16], T.pfb[:, XH:S]
            if who[0] == "g":
                op("g", lambda out=out: g.affine_select(out, src, [[0, S - XH]], ALU.is_gt, 0.0, 1, 0), [], ["pfx%d" % m], PFD)
            elif who[0] == "a":
                act(out, src, AF.Copy, [], ["pfx%d" % m], PFD)
            else:
                cp(out, src, [], ["pfx%d" % m], PFD)

    def select(out, src, pat, cmp, fill, base, cm, rd, wr):
        op("g", lambda: g.affine_select(out, src, pat, cmp, fill, base, cm), rd, wr)

    NC = (max(XA[0] + XA[1]) + 63) // 64

    def pool_constants():
        iota(T.blk[:, 8:16], [[0, 8]], 1, 0, ["blk1"])
        for i in range(2):
            select(T.pf2[:, i:128 * NC:2], T.pfb[:, 0:64 * NC], [[0, 64 * NC]], ALU.is_gt, 0.0, 1, 0, [], ["pf2%d" % i])
        select(T.blk[:, 0:8], T.blk[:, 8:16], [[-16, 8]], ALU.is_ge, 0.0, 0, 1, ["blk1"], ["blk0"])
        iota(T.wd[:], [[0, 144]], 0, 0, ["wd0"])
        select(T.blk[:, 8:16], T.blk[:, 0:8], [[16, 8]], ALU.is_ge, 0.0, 15, -1, ["blk0"], ["blk1"])
        iota(T.ax1[:], [[0, 384]], 0, 0, ["ax1"])
        select(T.wd[:, 15:143:16], T.blk[:, 8:16], [[0, 8]], ALU.is_gt, 0.0, 1, 0, ["blk1", "wd0"], ["wd"])
        iota(T.zero[:], [[0, 128]], 0, 0, ["zero"])
        for m in range(16 if XH > X0 else 0):
            select(T.pfx[:, m:16 * (XH - X0):16], T.pfb[:, X0:XH], [[0, XH - X0]], ALU.is_gt, 0.0, 1, 0, [], ["pfy%d" % m])
        select(T.pen1[:], T.zero[:], [[-16, 8], [0, 16]], ALU.is_ge, 4096.0, 0, 1, ["zero"], ["pen1"])
        select(T.pen[:], T.pen1[:], [[16, 8], [0, 16]], ALU.is_ge, 4096.0, 15, -1, ["pen1"], ["pen"])
        four, back = [[200, 4], [-16, 8], [-200, 4]], [[-200, 4], [16, 8], [200, 4]]
        select(T.sel4[:], T.zero[:], four, ALU.not_equal, 1.0, 0, 1, ["zero"], ["sel4"])
        select(T.pen1[:], T.zero[:], four, ALU.is_ge, 4096.0, 0, 1, ["zero"], ["pen1"])
        select(T.pen4[:], T.pen1[:], back, ALU.is_ge, 4096.0, 15, -1, ["pen1"], ["pen4"])
        iota(T.one[:, 0:1], [[0, 1]], 1, 0, ["one"])
        iota(T.pen32[:, 0:1], [[0, 1]], 0, 0, ["pen32128"])
        for q in range(0, 128, 32):
            select(T.pen32[q:q + 32, 1:33], T.pen[q:q + 32, q:q + 32], [[0, 32]], ALU.is_gt, 0.0, 1, 0, ["pen", "pen32128"], ["pen32%d" % q])

    def spread(ax, gs, rd, ext=()):
        tt(T[ax][:].indirect(T.offe[:, 0:3]), T[gs][:, 0:48], T[gs][:, 48:96], ALU.mult, rd + ["offe"], [ax], ext)

    def flags(t):
        act(T["live%d" % t][:], bk(COUNT[t][3]), AF.Copy, ["@" + COUNT[t][3]], ["live%d" % t])

    def lattices(t, pick, k, src):
        key, gs = ("sell", "win0")[t], "gs%d" % t
        b0, b2, b1, bl = COUNT[t]
        for bank in (b0, b2, b1):
            mm(bk(bank), pick, T.cum[0:k, :], False, True, [key, "cum", "!" + bank], ["@" + bank])
        if t == 0:
            mm(bk("y2"), T.sel[0:24, 256:384], T.posb[0:24, :], True, True, SELK + ["selr%d" % c for c in range(3)], ["@y2"])
        scan(T.sc[:, 0:S], bk(b0), T.ramp[:], ALU.min, ALU.max, ["@" + b0, "ramp"], ["sc0"])
        mm(bk(bl), pick, T[src][0:k, :], True, True, [key, src], ["@" + bl])
        act(T.junk[:], bk(b2), AF.Sign, ["@" + b2], ["cnt", "junk"], scale=-1.0, accum_out=T.cnt[:, 0:1])
        scan(T.sc[:, S:2 * S], bk(b1), T.ramp[:], ALU.min, ALU.max, ["@" + b1, "ramp"], ["sc1"])
        ts(T.offs[:, 0:6:5], T.k2[:, 0:2], T.cnt[:, 0:1], 0.5, ALU.add, ALU.mult, ["k2", "cnt"], ["offs0"])
        ts(T.offs[:, 1:3], T.sc[:, S - 1::S], -1024.0, None, ALU.mult, None, ["sc0", "sc1"], ["offs1"])
        ts(T.offs[:, 3:5], T.sc[:, S - 1::S], -1024.0, float(WB), ALU.mult, ALU.add, ["sc0", "sc1"], ["offs3"])
        if t == 0:
            cp(T.offe[:, 0:4], T.pci[:, 0:4], ["pci"], ["offe"])
            act(T.posr[:], bk("y2"), AF.Copy, ["@y2"], ["posr"])
        else:
            flags(t)
        cp(T[gs][:], T.w[:].indirect(T.offs[:, 0:6]), ["wa", "wb", "wz", "offs0", "offs1", "offs3"], [gs])
        if t == 0:
            ts(T.pc2[:, 0:1], T.pci[:, 0:1], 15, None, ALU.bitwise_and, None, ["pci"], ["m"])
        spread("ax0", gs, [gs])
        send(AXES[t], [AXES[t]])

    now = [0]

    def parts(J):
        x = XA[now[0]][J]
        return [(0, S)] if J else [(x, S), (0, x)]

    def span(J, blocks):
        xs, js = [x for p, j in blocks for x in parts(J)[p]], sorted(set(j for p, j in blocks))
        return (slice(None), slice(js[0], js[-1] + 1), slice(min(xs), max(xs))), ["@y%d" % j for j in js]

    def keys(kind, J, blocks):
        return ["%s%d%d%d" % (kind, J, p, j) for p, j in blocks]

    def every(J, axes):
        return [(p, j) for p in range(len(parts(J))) for j in axes]

    def dots(J, src, rd, ext=()):
        for j in (2, 0, 1):
            i = (j + 2) % 3
            mm(T.y[:, j, 0:S], T[src][:, 128 * i:128 * i + 128], T.posr[:], True, True, rd + ["posr"], ["@y%d" % j], ext)

    def floor_a(J, blocks, on):
        ix, yk = span(J, blocks)
        sc, bi = 1.0 / 2048, 192 - 511.5 / 2048
        if on == "a":
            act(T["ga%d" % J][ix], T.y[ix], AF.Copy, yk, keys("ga", J, blocks), bias=bi, scale=sc)
        else:
            ts(T["ga%d" % J][ix], T.y[ix], sc, bi, ALU.mult, ALU.add, yk, keys("ga", J, blocks))

    def floor_b(J, axes):
        ix, yk = span(J, every(J, axes))
        act(T["gb%d" % J][ix], T.y[ix], AF.Copy, yk, keys("gb", J, every(J, axes)), bias=-(192 + 512.5 / 2048), scale=-1.0 / 2048)

    def wrap(J, blocks, on):
        ix, yk = span(J, blocks)
        out, mod = T["f3%d" % J][ix], MOD[blocks[0][1]]
        if on == "a":
            act(out, T.y[ix], AF.Copy, yk, keys("f3", J, blocks), bias=-(512.5 / 2048 + 191.5 * mod), scale=-1.0 / 2048)
        else:
            ts(out, T["ga%d" % J][ix], -1.0, 192 - 192 * mod + (mod - 1) / 2, ALU.mult, ALU.add, keys("ga", J, blocks), keys("f3", J, blocks))

    def place_terms(J, p, order):
        x0, x1 = parts(J)[p]
        for i, (kind, j) in enumerate(order):
            mm(T.z[:, x0:x1], T[CID[j]][:], T["%s%d" % (kind, J)][:, j, x0:x1], i == 0, i == 5, [CID[j]] + keys(kind, J, [(p, j)]), ["@z"])

    def places(J, p):
        x0, x1 = parts(J)[p]
        c = sum(192 * COEF[j] * (MOD[j] - 1) for j in range(3))
        ts(T["off%d" % J][:, x0:x1], T.z[:, x0:x1], c, None, ALU.add, None, ["@z"], ["off%d%d" % (J, p)])

    def score_terms(J, kind, axes):
        for j in axes:
            mm(bk("s%d" % J), T.id8k[:], T["%s%d" % (kind, J)][:, j, :], False, False, ["id8k"] + keys(kind, J, every(J, [j])), ["@s%d" % J])

    def score_start(J, t, nb):
        mm(bk("s%d" % J), T.id8k[:], T["live%d" % t][:], True, False, ["id8k", "live%d" % t], ["@s%d" % J])
        score_terms(J, "ga", range(3))
        score_terms(J, "gb", range(nb))

    def verdict(J, name):
        act(T["nh%d" % J][:], bk("s%d" % J), AF.Sign, ["@s%d" % J, "thc"], ["nh%d" % J, name],
            bias=T.thc[:, 0:1], scale=-1.0, accum_out=T[name][:, 0:1])
        send(name, [name])

    def pieces(J, names, r=None):
        return ["pr%d%s%d" % (J, x, q) for x in names for q in (range(4) if r is None else [r])]

    def gather_a(J, name, x0, x1):
        act(T["pr%d" % J][:, 16 * x0:16 * x1], T.rfb[:].indirect(T["off%d" % J][:, x0:x1]), AF.Copy,
            ["off%d%d" % (J, len(parts(J)) - 1)], pieces(J, name), RF)

    def gather_v(J, name, x0, x1):
        tt(T["pr%d" % J][:, 16 * x0:16 * x1], T.rfb[:].indirect(T["off%d" % J][:, x0:x1]), T.pfx[:, 16 * (x0 - X0):16 * (x1 - X0)], ALU.mult,
           ["off%d0" % J] + ["pfx%d" % m for m in range(16)] + (["pfy%d" % m for m in range(16)] if x0 < XH else []), pieces(J, name), RF)

    def times(J, names, r, step, x0, x1):
        part, k = T["pr%d" % J][:, 16 * x0 + r:16 * x1:step], [p for q in range(r, 4, step) for p in pieces(J, names, q)]
        tt(part, part, T.pf8[:, 4 * x0:4 * x1:step // 2, :], ALU.mult, k + ["@pf8"], k)

    def turn_profiles():
        for c in range(NC):
            op("p", lambda c=c: P.transpose(T.pf8[:, 64 * c:64 * c + 64, :], T.pf2[:, 128 * c:128 * c + 128], T.id1[:]),
               ["pf20", "pf21", "id1"], ["@pf8"])
        cp(T.pft[:, 0:128 * NC], T.pf8[:, 0:64 * NC, :], ["@pf8"], ["pft"])

    def turn_back():
        for c in range(NC):
            for i in range(4):
                op("p", lambda c=c, i=i: P.transpose(T.pf8[:, 256 * c + i:256 * c + 256:4, :], T.pft[:, 128 * c:128 * c + 128], T.id1[:]),
                   ["pft", "id1"], ["@pf8"])

    def sums(J, names, r, bank, x0, x1, stop=True):
        for m in range(r, 16, 4):
            mm(bk(bank)[:, x0:x1], T.wd[:, 15 - m:143 - m], T["pr%d" % J][:, 16 * x0 + m:16 * x1:16], False, stop and m == 15,
               ["wd"] + pieces(J, names, r), ["@" + bank])

    def winner_early(J, one, ext=()):
        ts(T.tot[:, J:J + 1], T[one][:, 0:1], T.col[:, 3:4], None, ALU.add, None, ["col3"] + ([] if ext else [one]), ["tot%d" % J], ext)

    def winner(J, late, rd, pen, win, ext=()):
        key = "key%d" % J
        ts(T[key][:], T.pen32[:], T.tot[:, J:J + 1], late, ALU.add, ALU.add,
           ["pen32%d" % q for q in range(0, 129, 32)] + ["tot%d" % J] + rd, [key], ext)
        op("v", lambda: V.transpose(T.k32t[:], T[key][:, 1:33]), [key], ["k32t"])
        op("v", lambda: V.tensor_reduce(T.mn[:, 0:1], T.k32t[:], AX.X, ALU.min), ["k32t"], ["mn"])
        ts(T[win][:], T[pen][:], T[key][:, 0:1], T.mn[:, 0:1], ALU.add, ALU.is_le, [pen, "mn", key], [win])

    def limits():
        ts(T.thb[:, 0:1], T.thc[:, 0:1], -1.0, 3 * BIG, ALU.mult, ALU.add, ["thc"], ["thb0"])
        ts(T.col[:, 5:6], T.thc[:, 0:1], -1.0, 3 * BIG, ALU.mult, ALU.add, ["thc"], ["col5"])

    def limits_end():
        ts(T.col[:, 6:7], T.col[:, 5:6], T.thb[:, 0:1], None, ALU.subtract, None, ["col5", "thb0"], ["col6"])
        for i in range(2):
            ts(T.thd[:, 128 * i:128 * i + 128], T.id1[:], T.col[:, 5 + i:6 + i], None, ALU.mult, None, ["id1", "col%d" % (5 + i)], ["thd%d" % i])

    def turned(c):
        return (T.s1, "@s1") if c else (T.z, "@z")

    def turned_terms(c, nb):
        bank, key = turned(c)
        x, live = slice(128 * c, 128 * c + 128), "live%d" % now[0]
        for i in range(2):
            mm(bank[:, x], T[live][:, x], T.thd[:, 128 * i:128 * i + 128], i == 0 and c != 1, False, [live, "thd%d" % i], [key])
        for kind, j in [("ga", j) for j in range(3)] + [("gb", j) for j in range(nb)]:
            mm(bank[:, x], T[kind + "1"][:, j, x], T.id8k[:], False, False, ["id8k"] + keys(kind, 1, [(0, j)]), [key])

    def turned_late(nb):
        for c in (2, 1, 0):
            bank, key = turned(c)
            for j in range(nb, 3):
                mm(bank[:, 128 * c:128 * c + 128], T.gb1[:, j, 128 * c:128 * c + 128], T.id8k[:], False, False,
                   ["id8k"] + keys("gb", 1, [(0, j)]), [key])

    def turned_sums(names, c, residues):
        bank, key = turned(c)
        for r in residues:
            for m in range(r, 16, 4):
                mm(bank[:, 128 * c + m:128 * c + 128:16], T.pr1[:, 2048 * c + m:2048 * c + 2048:16], T.blk[:, 8:16], False, m == 15 and c < 2,
                   ["blk1"] + pieces(1, names, r), [key])

    def turned_verdict(chunks):
        bank, key = turned(chunks[0])
        x = slice(128 * chunks[0], 128 * chunks[-1] + 128)
        act(T.nt[:, x], bank[:, x], AF.Sign, [key], ["nt%d" % chunks[0]], bias=2 * BIG, scale=-1.0)

    def turned_back(chunks):
        k = "nt%d" % chunks[0]
        for c in chunks:
            mm(T.y[:, 0, 0:1], T.nt[:, 128 * c:128 * c + 128], T.one[:, 0:1], c == 1, c == 0, [k, "one"], ["@y0"])
        for c in chunks:
            mm(T.y[:, 1, 128 * c:128 * c + 128], T.nt[:, 128 * c:128 * c + 128], T.id1[:], True, True, [k, "id1"], ["@y1"])
        if chunks[0] == 0:
            act(T.nh1[:], bk("y1"), AF.Copy, ["@y1"], ["nh1"])

    def all_sums(J, names, x0, x1, stop=False):
        for r in range(4):
            sums(J, names, r, "s%d" % J, x0, x1, stop)

    def other_places():
        wrap(1, every(1, [0, 1]), "a")
        wrap(1, every(1, [2]), "a")
        place_terms(1, 0, [(k, j) for k in ("ga", "f3") for j in range(3)])

    def opening(J, ax, nb, first):
        dots(J, ax, [ax])
        floor_a(J, [(0, 2)], "v")
        floor_a(J, [(0, 0)], "a")
        floor_a(J, [(0, 1)], "a")
        wrap(J, [(0, 2)], "v")
        wrap(J, [(0, 0)], "v")
        wrap(J, [(0, 1)], "v")
        place_terms(J, 0, [("ga", 2), ("ga", 0), ("f3", 2), ("f3", 0), ("ga", 1), ("f3", 1)])
        floor_a(J, [(1, 2)], "v")
        if first:
            pfx_copies("a1")
        floor_a(J, [(1, 0), (1, 1)], "a")
        if first:
            pfx_copies("v1")
        wrap(J, [(1, 0), (1, 1)], "a")
        places(J, 0)
        wrap(J, [(1, 2)], "v")
        place_terms(J, 1, [("ga", 2), ("f3", 2), ("ga", 0), ("ga", 1), ("f3", 0), ("f3", 1)])
        if first:
            ts(T.id8k[:], T.uu[:], 0.0, BIG, ALU.is_equal, ALU.mult, ["uu"], ["id8k"])
        gather_v(J, "u", U, S)
        if first:
            flags(0)
        floor_b(J, range(nb))
        places(J, 1)

    pfx_copies("g0")
    early_b = 3 - LATE_B
    for t in range(RO):
        live, so, sf, ra, rb = ["%s%d" % (x, t) for x in ("live", "so", "sf", "ra", "rb")]
        if t == 0:
            lattices(0, T.sell[0:8, :], 8, "lvb")
            pfx_copies("g1")
            pool_constants()
            pfx_copies("a0")
            for j in (2, 0, 1):
                ts(T[CID[j]][:], T.uu[:], 0.0, COEF[j], ALU.is_equal, ALU.mult, ["uu"], [CID[j]])
            pfx_copies("v0")
        else:
            lattices(t, T.win0[:], 128, "surv")
        now[0] = t
        (xa0, xa1), ga, f0, f1, last = XA[t], GA, F0[t], F1, L[t]
        opening(0, "ax0", 3, t == 0)
        if t == 0:
            gather_a(0, "a", 0, xa0)
            ts(T.thc[:, 0:1], T.thi[:, 0:1], BIG - 0.5, None, ALU.add, None, [], ["thc"], TH)
            limits()
            turn_profiles()
            gather_v(0, "v", f0, U)
            score_start(0, t, 3)
            turn_back()
            spread("ax1", "rt0", [], came("rt0"))
            gather_v(0, "w", xa0, f0)
            dots(1, "ax1", ["ax1"])
            all_sums(0, "uv", f0, S)
            floor_a(1, every(1, range(3)), "a")
            other_places()
            floor_b(1, range(early_b))
            for r in range(2):
                times(0, "a", r, 2, 0, xa0)
            limits_end()
            columns()
            places(1, 0)
            all_sums(0, "aw", 0, f0, True)
            gather_v(1, "uv", 256, S)
            for c in (2, 1, 0):
                turned_terms(c, early_b)
        else:
            score_start(0, t, 0)
            gather_a(0, "a", 0, ga)
            gather_v(0, "v", f0, U)
            dots(1, "rt1", [], came("rt1"))
            score_terms(0, "gb", range(3))
            floor_a(1, every(1, range(3)), "a")
            other_places()
            places(1, 0)
            gather_a(0, "b", ga, xa0)
            gather_v(0, "w", xa0, f0)
            all_sums(0, "uv", f0, S)
            floor_b(1, range(early_b))
            gather_v(1, "u", f1, S)
            for r in range(2):
                times(0, "ab", r, 2, 0, xa0)
            turned_terms(2, early_b)
            all_sums(0, "abw", 0, f0, True)
            turned_terms(1, early_b)
            turned_terms(0, early_b)
            gather_v(1, "v", 256, f1)
        gather_a(1, "b", last, xa1)
        verdict(0, so)
        if LATE_B:
            floor_b(1, range(early_b, 3))
        gather_a(1, "c", 0, last)
        turned_sums("uv", 2, range(4))
        gather_v(1, "x", xa1, 256)
        turned_late(early_b)
        for r in range(2):
            times(1, "b", r, 2, last, xa1)
            turned_sums("bx", 1, (r, r + 2))
        turned_verdict((1, 2))
        for r in range(4):
            times(1, "c", r, 4, 0, last)
            turned_sums("bc", 0, [r])
        turned_back((1, 2))
        winner_early(0, so)
        turned_verdict((0,))
        turned_back((0,))
        cp(T[sf][:, 0:1], T.y[:, 0, 0:1], ["@y0"], [sf])
        send(sf, [sf])
        winner_early(1, ra, came(ra))
        mm(T.s0[:, 0:S], T.id8k[:], T[live][:], True, False, ["id8k", live], ["@s0"])
        mm(T.s0[:, 0:S], T.id1[:], T.nh0[:], False, False, ["id1", "nh0"], ["@s0"])
        Q = S // 4
        if t < RO - 1:
            thresholds(t + 1, range(3))
        else:
            for u in range(RO):
                for q in range(4):
                    mm(T.y[0:32, 0, 0:Q], T.sel4[:, 32 * q:32 * q + 32], T["live%d" % u][:, Q * q:Q * q + Q], u + q == 0, False,
                       ["sel4", "live%d" % u], ["@y0"])
        winner(1, T[sf][:, 0:1], [sf], "pen", "win1")
        mm(T.s0[:, 0:S], T.win1[:], T.nh1[:], False, True, ["win1", "nh1"], ["@s0"])
        if t < RO - 1:
            ts(T.surv[:], T.s0[:, 0:S], BIG + 1.5, None, ALU.is_ge, None, ["@s0"], ["surv"])
            scan(T.cum[:], T.surv[:], T.surv[:], ALU.add, ALU.max, ["surv"], ["cum"])
            winner(0, T[rb][:, 0:1], [], "pen", "win0", came(rb))
        else:
            act(T.junk[:], T.s0[:, 0:S], AF.Relu, ["@s0"], ["junk"], bias=-BIG - 1)
            winner(0, T[rb][:, 0:1], [], "pen4", "win4", came(rb))
            for q in range(4):
                mm(T.y[0:32, 0, 0:Q], T.win4[:, 32 * q:32 * q + 32], T.junk[:, Q * q:Q * q + Q], False, q == 3, ["win4", "junk"], ["@y0"])
        ts(T.ycs[:, t:t + 1], T.key0[:, 0:1], T.col[:, 4:5], -0.5, ALU.add, ALU.mult, ["key0", "col4"], ["ycs%d" % t])
    cp(T.yas[0:32, :], T.y[0:32, 0, 0:Q], ["@y0"], ["yas"])
    op("a", lambda: g.scalar.dma_start(T.yc[:], T.ycs[:, 0:RO]).then_inc(T.sem.d_out, 16), ["ycs%d" % t for t in range(RO)], [])
    op("s", lambda: g.sync.dma_start(T.ya[:], T.yas[0:32, :]).then_inc(T.sem.d_out, 16), ["yas"], [])
    emit(ops, {"v": V, "a": A, "p": P, "g": g, "s": g.sync}, T)
    g.sync.wait_ge(T.sem.d_out, 32)
    g.wait_ge(T.sem.sent, sent[0])
